import numpy as np
import ml_dtypes


def mxq(x, axis, fmt="e4m3"):
    dtype, down = {"e4m3": (ml_dtypes.float8_e4m3fn, 7), "e5m2": (ml_dtypes.float8_e5m2, 14)}[fmt]
    v = np.moveaxis(np.asarray(x, np.float32).astype(ml_dtypes.bfloat16).astype(np.float64), axis, -1)
    blocks = v.reshape(v.shape[:-1] + (-1, 32))
    amax = np.abs(blocks).max(-1, keepdims=True)
    byte = np.maximum(np.where(amax > 0, np.frexp(amax)[1] - 1 + 127, 0) - down, 1)
    scale = np.exp2(byte - 127.0)
    codes = (blocks / scale).astype(np.float32).astype(dtype).astype(np.float64)
    return np.moveaxis((codes * scale).reshape(v.shape), -1, axis)


WIDE = False


def mx_kscale(k):
    if not WIDE:
        return np.ones(k)
    levels = np.array([10, -10, 5, -5, 0])
    if k % 512:
        return np.exp2(np.random.permutation(np.resize(levels, k // 32))).repeat(32)
    a = np.empty((k // 512, 16))
    for p in range(k // 512):
        a[p, :8] = np.random.permutation(np.resize(levels, 8))
        for g in range(8):
            far = levels[np.abs(levels - a[p, g]) >= 10]
            a[p, g + 8] = far[np.random.randint(len(far))]
    return np.exp2(a.ravel()).repeat(32)


def f64(x):
    return np.asarray(x).astype(np.float64)


def striped(idx):
    return np.tile(idx.reshape(-1, 16).T, (8, 1)).astype(np.uint16)


def unstriped(offs):
    return offs[:16].T.reshape(-1).astype(np.int64)


E2M1 = np.array([0.0, 0.5, 1.0, 1.5, 2.0, 3.0, 4.0, 6.0, -0.0, -0.5, -1.0, -1.5, -2.0, -3.0, -4.0, -6.0])


def pack_weight(w, fmt):
    k, n = w.shape
    w = f64(np.asarray(w, np.float32).astype(ml_dtypes.bfloat16)).reshape(k // 32, 32, n)
    amax = np.abs(w).max(1)
    if fmt == "e4m3":
        byte = np.frexp(amax)[1] - 1 + 127 - 7
    else:
        mant, ex = np.frexp(amax / 6.0)
        byte = np.where(mant > 0.5, ex, ex - 1) + 127
    byte = np.clip(np.where(amax > 0, byte, 1), 1, 254)
    scaled = (w * np.exp2(127.0 - byte)[:, None, :]).reshape(k, n).astype(np.float32)
    by_word = np.ascontiguousarray(scaled.reshape(k // 512, 128, 4, n).transpose(0, 1, 3, 2))
    if fmt == "e4m3":
        words = by_word.astype(ml_dtypes.float8_e4m3fn).view(np.uint8)
    else:
        c = by_word.astype(ml_dtypes.float4_e2m1fn).view(np.uint8) & 0xF
        words = (c[..., 0::2] | (c[..., 1::2] << 4)).reshape(k // 512, 128, 2 * n)
    return np.ascontiguousarray(words), np.ascontiguousarray(byte.astype(np.uint8).reshape(k // 512, 16, n))


def unpack_weight(words, scales, fmt):
    g, _, n = scales.shape
    words = np.ascontiguousarray(words).reshape(g, 128, n, -1)
    if fmt == "e4m3":
        vals = words.view(ml_dtypes.float8_e4m3fn).astype(np.float64)
    else:
        nib = np.empty((g, 128, n, 4), np.uint8)
        nib[..., 0::2] = words & 0xF
        nib[..., 1::2] = words >> 4
        vals = E2M1[nib]
    vals = vals * np.repeat(np.exp2(scales.astype(np.float64) - 127.0), 8, axis=1)[..., None]
    return vals.transpose(0, 1, 3, 2).reshape(g * 512, n)


def gelu(v):
    return 0.5 * v * (1.0 + np.tanh(np.sqrt(2.0 / np.pi) * (v + 0.044715 * v**3)))


def striped8(idx):
    return np.concatenate([v.reshape(-1, 16).T for v in idx]).astype(np.uint16)


def unstriped8(offs):
    return np.stack([offs[16 * g:16 * g + 16].T.reshape(-1) for g in range(8)]).astype(np.int64)


def runs(v, idx8):
    k = np.arange(v.shape[0])
    return v[k[:, None], idx8[k % 512 // 64]]


K, K2, H, N, T, S = 1024, 512, 1024, 512, 2048, 1024

def setup_inputs():
    n = np.random.standard_normal
    s = mx_kscale(K)[:, None]
    s2 = mx_kscale(K2)[:, None]
    u = mx_kscale(H)[:, None]
    tab_words, tab_scales = pack_weight(n((K, T)) * s, "e4m3")
    tab2_words, tab2_scales = pack_weight(n((K2, T)) * s2, "e4m3")
    w4_words, w4_scales = pack_weight(1.5 * n((K2, H)) / np.sqrt(K2) / s2, "e2m1")
    w8_words, w8_scales = pack_weight(3.0 * n((H, N)) / np.sqrt(H) / u, "e4m3")
    return {
        "tab_words": tab_words, "tab_scales": tab_scales,
        "tab2_words": tab2_words, "tab2_scales": tab2_scales,
        "offs": striped8(np.stack([np.random.permutation(T)[:S] for _ in range(8)])),
        "offs2": striped(np.random.permutation(T)[:S]),
        "w1": (1.5 * n((K, H)) / np.sqrt(K) / s).astype(np.float32),
        "w4_words": w4_words, "w4_scales": w4_scales,
        "gain": (np.exp(0.3 * n(H)) * u[:, 0]).astype(np.float32),
        "w8_words": w8_words, "w8_scales": w8_scales,
    }

def reference(tab_words, tab_scales, tab2_words, tab2_scales, offs, offs2, w1, w4_words, w4_scales, gain, w8_words, w8_scales):
    v = runs(unpack_weight(tab_words, tab_scales, "e4m3"), unstriped8(offs))
    v2 = unpack_weight(tab2_words, tab2_scales, "e4m3")[:, unstriped(offs2)]
    a = mxq(f64(w1), 0, "e4m3").T @ v
    b = unpack_weight(w4_words, w4_scales, "e2m1").T @ v2
    tissue = 1 / (1 + np.exp(-a))
    unlike = 1 / (1 + np.exp(b))
    h = tissue * unlike * f64(gain)[:, None]
    y = unpack_weight(w8_words, w8_scales, "e4m3").T @ mxq(h, 0, "e4m3")
    return y / (1 + np.abs(y))

@@ -1,0 +1,247 @@
+from contextlib import ExitStack
+
+import concourse.mybir as mybir
+
+K, K2, H, N, T, S = 1024, 512, 1024, 512, 2048, 1024
+FLOPS = 2 * S * (K * H + K2 * H + H * N)
+
+F32 = mybir.dt.float32
+BF16 = mybir.dt.bfloat16
+I32 = mybir.dt.int32
+U32 = mybir.dt.uint32
+U16 = mybir.dt.uint16
+U8 = mybir.dt.uint8
+FP8X4 = mybir.dt.float8_e4m3fn_x4
+FP4X4 = mybir.dt.float4_e2m1fn_x4
+ACT = mybir.ActivationFunctionType
+ALU = mybir.AluOpType
+
+P = 128
+PACK = 4
+PASS = P * PACK
+JW = 512
+HALVES = S // JW
+GROUPS = H // PASS
+PASSES = K // PASS
+PLANE_ROW = 8
+
+
+def tile_list_tissue_share_scores_kernel(
+    tc, tab_words, tab_scales, tab2_words, tab2_scales, offs, offs2, w1, w4_words, w4_scales, gain, w8_words, w8_scales, out
+):
+    nc = tc.nc
+    with ExitStack() as ctx:
+        keep = ctx.enter_context(tc.tile_pool(name="keep", bufs=1))
+        ring = ctx.enter_context(tc.tile_pool(name="ring", bufs=2))
+        psum = ctx.enter_context(tc.psum_pool(name="psum", bufs=4))
+
+        def held(shape, dtype, name):
+            return keep.tile(shape, dtype, name=name, align_bytes=64)
+
+        lists = keep.tile([P, S // 16], U16, name="lists")
+        list2 = keep.tile([P, S // 16], U16, name="list2")
+        tab_rows = keep.tile([P, T], U8, name="tab_rows", tag="slot_c", align_bytes=64)
+        tab2_rows = keep.tile([P, T], U8, name="tab2_rows", tag="slot_e", align_bytes=64)
+        warm_in = keep.tile([P, 1], F32, name="warm_in", tag="slot_b", align_bytes=64)
+        warm_out = keep.tile([P, 1], F32, name="warm_out", tag="slot_f", align_bytes=64)
+
+        nc.vector.memset(tab_rows[:].bitcast(I32), 0)
+        nc.vector.memset(tab2_rows[:].bitcast(I32), 0)
+        nc.vector.memset(warm_in[:], 0.0)
+        nc.scalar.activation(warm_out[:], warm_in[:], ACT.Sigmoid)
+        weight_rows = keep.tile([P, H], U8, name="weight_rows", tag="slot_f", align_bytes=64)
+        nc.vector.memset(weight_rows[:].bitcast(I32), 0)
+
+        def load_w1(g, a, tag):
+            raw = keep.tile([P, PACK, PASS], F32, name="w1_raw", tag=tag, align_bytes=64)
+            rows = w1[PASS * a : PASS * (a + 1), PASS * g : PASS * (g + 1)]
+            nc.sync.dma_start(raw[:], rows.rearrange("(p j) c -> p j c", j=PACK))
+            return raw
+
+        def load_words(words, tag):
+            table = keep.tile([P, T], I32, name="table", tag=tag, align_bytes=64)
+            nc.sync.dma_start(table[:], words.rearrange("p t i -> p (t i)").bitcast(I32))
+            return table
+
+        for i in range(2):
+            nc.sync.dma_start(
+                tab_rows[:].bitcast(I32)[i:P:PLANE_ROW, :],
+                tab_scales.bitcast(I32)[:, i:16:2, :].rearrange("a g t -> g a t"),
+            )
+        for r in range(4):
+            nc.sync.dma_start(tab2_rows[:].bitcast(I32)[r:P:32, :], tab2_scales.bitcast(I32)[0, r:16:4, :])
+        nc.sync.dma_start(lists[:], offs)
+        nc.sync.dma_start(list2[:], offs2)
+        w4_raw = keep.tile([P, 2 * H], U8, name="w4_raw", tag="tab_early", align_bytes=64)
+        nc.sync.dma_start(w4_raw[:].bitcast(I32), w4_words.bitcast(I32)[0])
+        gains = held([P, GROUPS, PACK], F32, "gains")
+        nc.sync.dma_start(gains[:], gain.rearrange("(g p t) -> p g t", g=GROUPS, t=PACK))
+        w1_raw = {}
+        tab2 = load_words(tab2_words[0], "slot_d")
+        w1_raw[0, 0] = load_w1(0, 0, "slot_a")
+        w1_raw[0, 1] = load_w1(0, 1, "slot_b")
+        for r in range(4):
+            nc.sync.dma_start(weight_rows[:].bitcast(I32)[r:P:32, :], w4_scales.bitcast(I32)[0, r:16:4, :])
+
+        w4 = held([P, 2 * H], U8, "w4")
+        nc.vector.tensor_copy(
+            w4[:].bitcast(U16).rearrange("p (g t m) -> p g t m", g=GROUPS, t=PACK),
+            w4_raw[:].bitcast(U16).rearrange("p (g m t) -> p g t m", g=GROUPS, t=PACK),
+        )
+        tab = {0: load_words(tab_words[0], "tab_early")}
+
+        def gather_words(table, offsets, half, name):
+            picked = held([P, JW], U32, name)
+            part = offsets[:, half * (JW // 16) : (half + 1) * (JW // 16)]
+            nc.vector.tensor_copy(picked[:], table[:].bitcast(U32).indirect(part))
+            return picked
+
+        v2 = [gather_words(tab2, list2, half, "v2_%d" % half) for half in range(HALVES)]
+        tab[1] = load_words(tab_words[1], "slot_d")
+        v_rows = held([P, S], U8, "v_rows")
+        nc.vector.tensor_copy(v_rows[:], tab_rows[:].indirect(lists[:]))
+        v_plane = held([P, S], U8, "v_plane")
+        nc.vector.tensor_copy(v_plane[:].bitcast(I32), v_rows[:].bitcast(I32))
+        for i in range(2):
+            nc.scalar.dma_start(
+                v_plane[:].bitcast(I32)[2 + i : P - 16 + 2 : PLANE_ROW, :],
+                v_rows[:].bitcast(I32)[16 + i : P : PLANE_ROW, :],
+            )
+        v2_plane = held([P, S], U8, "v2_plane")
+        nc.vector.tensor_copy(v2_plane[:], tab2_rows[:].indirect(list2[:]))
+        w4_plane = held([P, H], U8, "w4_plane")
+        nc.vector.tensor_copy(
+            w4_plane[:].rearrange("p (g t m) -> p g t m", g=GROUPS, t=PACK),
+            weight_rows[:].rearrange("p (g m t) -> p g t m", g=GROUPS, t=PACK),
+        )
+
+        w1_codes, w1_plane, w1_bf = {}, {}, {}
+
+        def round_w1(g, a, on_scalar):
+            grouped = held([P, PACK * PASS], BF16, "w1_bf%d%d" % (g, a))
+            dst = grouped[:].rearrange("p (t m j) -> p m j t", t=PACK, j=PACK)
+            src = w1_raw[g, a][:].rearrange("p j (m t) -> p m j t", t=PACK)
+            if on_scalar:
+                nc.scalar.copy(dst, src)
+            else:
+                nc.vector.tensor_copy(dst, src)
+            w1_bf[g, a] = grouped
+
+        def quantize_w1(g, a):
+            w1_codes[g, a] = held([P, PASS], U32, "w1_codes%d%d" % (g, a))
+            w1_plane[g, a] = held([P, PASS], U8, "w1_plane%d%d" % (g, a))
+            nc.vector.quantize_mx(out=w1_codes[g, a][:].bitcast(FP8X4), scales=w1_plane[g, a][:], in_=w1_bf[g, a][:])
+
+        unlike, tissue = {}, {}
+
+        def control_product(g, half, t):
+            col = PASS * g + P * t
+            b = psum.tile([P, JW], F32, name="b", tag="first")
+            nc.tensor.matmul_mx(
+                out=b[:],
+                lhsT=w4[:, 2 * col : 2 * (col + P)].bitcast(FP4X4),
+                lhsT_scale=w4_plane[:, col : col + P],
+                rhs=v2[half][:].bitcast(FP8X4),
+                rhs_scale=v2_plane[:, JW * half : JW * (half + 1)],
+                start=True,
+                stop=True,
+            )
+            tag = "slot_b" if (g, half, t) == (0, 0, 0) else "unlike%d%d%d" % (g, half, t)
+            unlike[g, half, t] = keep.tile([P, JW], F32, name="unlike", tag=tag, align_bytes=64)
+            nc.scalar.activation(unlike[g, half, t][:], b[:], ACT.Sigmoid, scale=-1.0)
+
+        v = {}
+
+        def tissue_product(g, half, t):
+            acc = psum.tile([P, JW], F32, name="acc", tag="first")
+            for a in range(PASSES):
+                nc.tensor.matmul_mx(
+                    out=acc[:],
+                    lhsT=w1_codes[g, a][:, P * t : P * (t + 1)].bitcast(FP8X4),
+                    lhsT_scale=w1_plane[g, a][:, P * t : P * (t + 1)],
+                    rhs=v[a, half][:].bitcast(FP8X4),
+                    rhs_scale=v_plane[PLANE_ROW * a : P, JW * half : JW * (half + 1)],
+                    start=(a == 0),
+                    stop=(a == PASSES - 1),
+                )
+            tissue[g, half, t] = ring.tile([P, JW], F32, name="tissue", bufs=12)
+            nc.scalar.activation(tissue[g, half, t][:], acc[:], ACT.Sigmoid)
+
+        h_codes, h_plane = {}, {}
+
+        def make_h(g, half):
+            slots = ring.tile([P, PACK, JW], BF16, name="slots", align_bytes=64)
+            for t in range(PACK):
+                nc.vector.scalar_tensor_tensor(
+                    slots[:, t, :], tissue[g, half, t][:], gains[:, g, t : t + 1], unlike[g, half, t][:], ALU.mult, ALU.mult
+                )
+            woven = ring.tile([P, PACK * JW], BF16, name="woven", align_bytes=64)
+            nc.vector.tensor_copy(
+                woven[:].rearrange("p (c i t) -> p c t i", i=4, t=PACK),
+                slots[:].rearrange("p t (c i) -> p c t i", i=4),
+            )
+            h_codes[g, half] = held([P, JW], U32, "h_codes%d%d" % (g, half))
+            h_plane[g, half] = held([P, JW], U8, "h_plane%d%d" % (g, half))
+            nc.vector.quantize_mx(out=h_codes[g, half][:].bitcast(FP8X4), scales=h_plane[g, half][:], in_=woven[:])
+
+        def scores(half, tag, squares):
+            for n in range(N // P):
+                y = psum.tile([P, JW], F32, name="y", tag=tag)
+                for g in range(GROUPS):
+                    nc.tensor.matmul_mx(
+                        out=y[:],
+                        lhsT=w8[:, g, P * n : P * (n + 1)].bitcast(FP8X4),
+                        lhsT_scale=weight_rows[4 * g : P, P * n : P * (n + 1)],
+                        rhs=h_codes[g, half][:].bitcast(FP8X4),
+                        rhs_scale=h_plane[g, half][:],
+                        start=(g == 0),
+                        stop=(g == GROUPS - 1),
+                    )
+                size = ring.tile([P, JW], F32, name="size")
+                nc.scalar.activation(size[:], y[:], ACT.Abs)
+                root = ring.tile([P, JW], F32, name="root", bufs=4)
+                nc.scalar.activation(root[:], size[:], ACT.Abs_reciprocal_sqrt, bias=1.0)
+                part = ring.tile([P, JW], F32, name="part", bufs=4)
+                score = held([P, JW], F32, "score%d%d" % (half, n))
+                if n < squares:
+                    nc.scalar.activation(part[:], root[:], ACT.Square)
+                    nc.vector.tensor_tensor(score[:], y[:], part[:], ALU.mult)
+                else:
+                    nc.vector.tensor_tensor(part[:], y[:], root[:], ALU.mult)
+                    nc.vector.tensor_tensor(score[:], part[:], root[:], ALU.mult)
+                nc.sync.dma_start(out[P * n : P * (n + 1), JW * half : JW * (half + 1)], score[:])
+
+        for a in range(PASSES):
+            round_w1(0, a, True)
+            quantize_w1(0, a)
+        w1_raw[1, 0] = load_w1(1, 0, "slot_c")
+        w1_raw[1, 1] = load_w1(1, 1, "slot_a")
+        w8 = keep.tile([P, GROUPS, N], I32, name="w8", tag="slot_e", align_bytes=64)
+        nc.sync.dma_start(w8[:], w8_words.rearrange("g p c i -> p g (c i)").bitcast(I32))
+        for d in range(4):
+            nc.sync.dma_start(
+                weight_rows[:].bitcast(I32)[32 * d : 32 * d + 4 * GROUPS, 0 : N // 4],
+                w8_scales.bitcast(I32)[:, 4 * d : 4 * d + 4, :],
+            )
+        for half in range(HALVES):
+            for t in range(PACK):
+                control_product(0, half, t)
+        for half in range(HALVES):
+            for a in range(PASSES):
+                v[a, half] = gather_words(tab[a], lists, half, "v%d%d" % (a, half))
+        for half in range(HALVES):
+            for t in range(PACK):
+                tissue_product(0, half, t)
+        make_h(0, 0)
+        for a in range(PASSES):
+            round_w1(1, a, a == 0)
+            quantize_w1(1, a)
+        make_h(0, 1)
+        for half in range(HALVES):
+            for t in range(PACK):
+                control_product(1, half, t)
+                tissue_product(1, half, t)
+        make_h(1, 0)
+        make_h(1, 1)
+        scores(0, "second", 2)
+        scores(1, "first", 0)

@@ -33,23 +33,22 @@ def tile_list_tissue_share_scores_kernel(
     with ExitStack() as ctx:
         keep = ctx.enter_context(tc.tile_pool(name="keep", bufs=1))
         ring = ctx.enter_context(tc.tile_pool(name="ring", bufs=2))
-        psum = ctx.enter_context(tc.psum_pool(name="psum", bufs=4))
+        psum = ctx.enter_context(tc.psum_pool(name="psum", bufs=1))
 
         def held(shape, dtype, name):
             return keep.tile(shape, dtype, name=name, align_bytes=64)
 
         lists = keep.tile([P, S // 16], U16, name="lists")
         list2 = keep.tile([P, S // 16], U16, name="list2")
-        tab_rows = keep.tile([P, T], U8, name="tab_rows", tag="slot_c", align_bytes=64)
-        tab2_rows = keep.tile([P, T], U8, name="tab2_rows", tag="slot_e", align_bytes=64)
-        warm_in = keep.tile([P, 1], F32, name="warm_in", tag="slot_b", align_bytes=64)
-        warm_out = keep.tile([P, 1], F32, name="warm_out", tag="slot_f", align_bytes=64)
+        tab2_rows = held([P, T], U8, "tab2_rows")
+        tab_rows = held([P, T], U8, "tab_rows")
+        weight_rows = held([P, H], U8, "weight_rows")
+        warm = held([P, 2], F32, "warm")
 
         nc.vector.memset(tab_rows[:].bitcast(I32), 0)
+        nc.vector.memset(warm[:, 0:1], 0.0)
+        nc.scalar.activation(warm[:, 1:2], warm[:, 0:1], ACT.Sigmoid)
         nc.vector.memset(tab2_rows[:].bitcast(I32), 0)
-        nc.vector.memset(warm_in[:], 0.0)
-        nc.scalar.activation(warm_out[:], warm_in[:], ACT.Sigmoid)
-        weight_rows = keep.tile([P, H], U8, name="weight_rows", tag="slot_f", align_bytes=64)
         nc.vector.memset(weight_rows[:].bitcast(I32), 0)
 
         def load_w1(g, a, tag):
@@ -63,32 +62,46 @@ def tile_list_tissue_share_scores_kernel(
             nc.sync.dma_start(table[:], words.rearrange("p t i -> p (t i)").bitcast(I32))
             return table
 
+        nc.sync.dma_start(lists[:], offs)
         for i in range(2):
             nc.sync.dma_start(
                 tab_rows[:].bitcast(I32)[i:P:PLANE_ROW, :],
                 tab_scales.bitcast(I32)[:, i:16:2, :].rearrange("a g t -> g a t"),
             )
+        w1_raw = {}
+        w1_raw[0, 0] = load_w1(0, 0, "raw00")
+        nc.sync.dma_start(list2[:], offs2)
         for r in range(4):
             nc.sync.dma_start(tab2_rows[:].bitcast(I32)[r:P:32, :], tab2_scales.bitcast(I32)[0, r:16:4, :])
-        nc.sync.dma_start(lists[:], offs)
-        nc.sync.dma_start(list2[:], offs2)
-        w4_raw = keep.tile([P, 2 * H], U8, name="w4_raw", tag="tab_early", align_bytes=64)
+        w4_raw = held([P, 2 * H], U8, "w4_raw")
         nc.sync.dma_start(w4_raw[:].bitcast(I32), w4_words.bitcast(I32)[0])
-        gains = held([P, GROUPS, PACK], F32, "gains")
-        nc.sync.dma_start(gains[:], gain.rearrange("(g p t) -> p g t", g=GROUPS, t=PACK))
-        w1_raw = {}
-        tab2 = load_words(tab2_words[0], "slot_d")
-        w1_raw[0, 0] = load_w1(0, 0, "slot_a")
-        w1_raw[0, 1] = load_w1(0, 1, "slot_b")
+        w1_raw[0, 1] = load_w1(0, 1, "raw01")
         for r in range(4):
             nc.sync.dma_start(weight_rows[:].bitcast(I32)[r:P:32, :], w4_scales.bitcast(I32)[0, r:16:4, :])
+        tab2 = load_words(tab2_words[0], "tab2")
+        tab = [load_words(tab_words[a], "tab%d" % a) for a in range(PASSES)]
 
+        v_rows = held([P, S], U8, "v_rows")
+        nc.vector.tensor_copy(v_rows[:], tab_rows[:].indirect(lists[:]))
+        v_plane = held([P, S], U8, "v_plane")
+        nc.vector.tensor_copy(v_plane[:].bitcast(I32), v_rows[:].bitcast(I32))
+        for i in range(2):
+            nc.sync.dma_start(
+                v_plane[:].bitcast(I32)[2 + i : P - 16 + 2 : PLANE_ROW, :],
+                v_rows[:].bitcast(I32)[16 + i : P : PLANE_ROW, :],
+            )
+        v2_plane = held([P, S], U8, "v2_plane")
+        nc.vector.tensor_copy(v2_plane[:], tab2_rows[:].indirect(list2[:]))
         w4 = held([P, 2 * H], U8, "w4")
         nc.vector.tensor_copy(
             w4[:].bitcast(U16).rearrange("p (g t m) -> p g t m", g=GROUPS, t=PACK),
             w4_raw[:].bitcast(U16).rearrange("p (g m t) -> p g t m", g=GROUPS, t=PACK),
         )
-        tab = {0: load_words(tab_words[0], "tab_early")}
+        w4_plane = held([P, H], U8, "w4_plane")
+        nc.vector.tensor_copy(
+            w4_plane[:].rearrange("p (g t m) -> p g t m", g=GROUPS, t=PACK),
+            weight_rows[:].rearrange("p (g m t) -> p g t m", g=GROUPS, t=PACK),
+        )
 
         def gather_words(table, offsets, half, name):
             picked = held([P, JW], U32, name)
@@ -97,28 +110,25 @@ def tile_list_tissue_share_scores_kernel(
             return picked
 
         v2 = [gather_words(tab2, list2, half, "v2_%d" % half) for half in range(HALVES)]
-        tab[1] = load_words(tab_words[1], "slot_d")
-        v_rows = held([P, S], U8, "v_rows")
-        nc.vector.tensor_copy(v_rows[:], tab_rows[:].indirect(lists[:]))
-        v_plane = held([P, S], U8, "v_plane")
-        nc.vector.tensor_copy(v_plane[:].bitcast(I32), v_rows[:].bitcast(I32))
-        for i in range(2):
-            nc.scalar.dma_start(
-                v_plane[:].bitcast(I32)[2 + i : P - 16 + 2 : PLANE_ROW, :],
-                v_rows[:].bitcast(I32)[16 + i : P : PLANE_ROW, :],
+        w1_raw[1, 0] = load_w1(1, 0, "raw10")
+        w1_raw[1, 1] = load_w1(1, 1, "raw11")
+        gains = held([P, GROUPS, PACK], F32, "gains")
+        nc.sync.dma_start(gains[:], gain.rearrange("(g p t) -> p g t", g=GROUPS, t=PACK))
+        w8 = keep.tile([P, GROUPS, N], I32, name="w8", tag="tab2", align_bytes=64)
+        nc.sync.dma_start(w8[:], w8_words.rearrange("g p c i -> p g (c i)").bitcast(I32))
+        for d in range(4):
+            nc.sync.dma_start(
+                weight_rows[:].bitcast(I32)[32 * d : 32 * d + 4 * GROUPS, 0 : N // 4],
+                w8_scales.bitcast(I32)[:, 4 * d : 4 * d + 4, :],
             )
-        v2_plane = held([P, S], U8, "v2_plane")
-        nc.vector.tensor_copy(v2_plane[:], tab2_rows[:].indirect(list2[:]))
-        w4_plane = held([P, H], U8, "w4_plane")
-        nc.vector.tensor_copy(
-            w4_plane[:].rearrange("p (g t m) -> p g t m", g=GROUPS, t=PACK),
-            weight_rows[:].rearrange("p (g m t) -> p g t m", g=GROUPS, t=PACK),
-        )
+
+        def bank(number):
+            return psum.tile([P, JW], F32, name="bank", tag="bank%d" % number)
 
         w1_codes, w1_plane, w1_bf = {}, {}, {}
 
         def round_w1(g, a, on_scalar):
-            grouped = held([P, PACK * PASS], BF16, "w1_bf%d%d" % (g, a))
+            grouped = keep.tile([P, PACK * PASS], BF16, name="grouped", tag="w1_bf%d%d" % (g, a), align_bytes=64)
             dst = grouped[:].rearrange("p (t m j) -> p m j t", t=PACK, j=PACK)
             src = w1_raw[g, a][:].rearrange("p j (m t) -> p m j t", t=PACK)
             if on_scalar:
@@ -136,7 +146,7 @@ def tile_list_tissue_share_scores_kernel(
 
         def control_product(g, half, t):
             col = PASS * g + P * t
-            b = psum.tile([P, JW], F32, name="b", tag="first")
+            b = bank(t)
             nc.tensor.matmul_mx(
                 out=b[:],
                 lhsT=w4[:, 2 * col : 2 * (col + P)].bitcast(FP4X4),
@@ -146,14 +156,14 @@ def tile_list_tissue_share_scores_kernel(
                 start=True,
                 stop=True,
             )
-            tag = "slot_b" if (g, half, t) == (0, 0, 0) else "unlike%d%d%d" % (g, half, t)
+            tag = "unlike%d%d%d" % (g, half, t)
             unlike[g, half, t] = keep.tile([P, JW], F32, name="unlike", tag=tag, align_bytes=64)
             nc.scalar.activation(unlike[g, half, t][:], b[:], ACT.Sigmoid, scale=-1.0)
 
         v = {}
 
         def tissue_product(g, half, t):
-            acc = psum.tile([P, JW], F32, name="acc", tag="first")
+            acc = bank(t)
             for a in range(PASSES):
                 nc.tensor.matmul_mx(
                     out=acc[:],
@@ -169,8 +179,8 @@ def tile_list_tissue_share_scores_kernel(
 
         h_codes, h_plane = {}, {}
 
-        def make_h(g, half):
-            slots = ring.tile([P, PACK, JW], BF16, name="slots", align_bytes=64)
+        def make_h(g, half, tag):
+            slots = keep.tile([P, PACK, JW], BF16, name="slots", tag=tag, align_bytes=64)
             for t in range(PACK):
                 nc.vector.scalar_tensor_tensor(
                     slots[:, t, :], tissue[g, half, t][:], gains[:, g, t : t + 1], unlike[g, half, t][:], ALU.mult, ALU.mult
@@ -184,9 +194,9 @@ def tile_list_tissue_share_scores_kernel(
             h_plane[g, half] = held([P, JW], U8, "h_plane%d%d" % (g, half))
             nc.vector.quantize_mx(out=h_codes[g, half][:].bitcast(FP8X4), scales=h_plane[g, half][:], in_=woven[:])
 
-        def scores(half, tag, squares):
+        def scores(half, first_bank, squares):
             for n in range(N // P):
-                y = psum.tile([P, JW], F32, name="y", tag=tag)
+                y = bank(first_bank + n)
                 for g in range(GROUPS):
                     nc.tensor.matmul_mx(
                         out=y[:],
@@ -203,7 +213,7 @@ def tile_list_tissue_share_scores_kernel(
                 nc.scalar.activation(root[:], size[:], ACT.Abs_reciprocal_sqrt, bias=1.0)
                 part = ring.tile([P, JW], F32, name="part", bufs=4)
                 score = held([P, JW], F32, "score%d%d" % (half, n))
-                if n < squares:
+                if n >= N // P - squares:
                     nc.scalar.activation(part[:], root[:], ACT.Square)
                     nc.vector.tensor_tensor(score[:], y[:], part[:], ALU.mult)
                 else:
@@ -214,34 +224,28 @@ def tile_list_tissue_share_scores_kernel(
         for a in range(PASSES):
             round_w1(0, a, True)
             quantize_w1(0, a)
-        w1_raw[1, 0] = load_w1(1, 0, "slot_c")
-        w1_raw[1, 1] = load_w1(1, 1, "slot_a")
-        w8 = keep.tile([P, GROUPS, N], I32, name="w8", tag="slot_e", align_bytes=64)
-        nc.sync.dma_start(w8[:], w8_words.rearrange("g p c i -> p g (c i)").bitcast(I32))
-        for d in range(4):
-            nc.sync.dma_start(
-                weight_rows[:].bitcast(I32)[32 * d : 32 * d + 4 * GROUPS, 0 : N // 4],
-                w8_scales.bitcast(I32)[:, 4 * d : 4 * d + 4, :],
-            )
-        for half in range(HALVES):
+        for g, half in ((0, 0), (0, 1), (1, 0)):
             for t in range(PACK):
-                control_product(0, half, t)
+                control_product(g, half, t)
         for half in range(HALVES):
             for a in range(PASSES):
                 v[a, half] = gather_words(tab[a], lists, half, "v%d%d" % (a, half))
         for half in range(HALVES):
             for t in range(PACK):
                 tissue_product(0, half, t)
-        make_h(0, 0)
         for a in range(PASSES):
-            round_w1(1, a, a == 0)
+            round_w1(1, a, False)
             quantize_w1(1, a)
-        make_h(0, 1)
-        for half in range(HALVES):
-            for t in range(PACK):
-                control_product(1, half, t)
-                tissue_product(1, half, t)
-        make_h(1, 0)
-        make_h(1, 1)
-        scores(0, "second", 2)
-        scores(1, "first", 0)
+        make_h(0, 0, "raw11")
+        for t in range(PACK):
+            tissue_product(1, 0, t)
+        for t in range(PACK):
+            control_product(1, 1, t)
+        for t in range(PACK):
+            tissue_product(1, 1, t)
+        nc.scalar.activation(warm[:, 1:2], tissue[1, 1, PACK - 1][:, 0:1], ACT.Abs_reciprocal_sqrt, bias=1.0)
+        make_h(1, 0, "raw10")
+        scores(0, 4, 4)
+        make_h(0, 1, "raw10")
+        make_h(1, 1, "raw11")
+        scores(1, 0, 2)

@@ -42,14 +42,22 @@ def tile_list_tissue_share_scores_kernel(
         list2 = keep.tile([P, S // 16], U16, name="list2")
         tab2_rows = held([P, T], U8, "tab2_rows")
         tab_rows = held([P, T], U8, "tab_rows")
-        weight_rows = held([P, H], U8, "weight_rows")
+        w4_rows = keep.tile([P, H], U8, name="w4_rows", tag="w4_rows", align_bytes=64)
+        w8_plane = held([P, N], U8, "w8_plane")
         warm = held([P, 2], F32, "warm")
 
+        nc.gpsimd.memset(tab2_rows[:].bitcast(I32), 0)
+        nc.vector.memset(w4_rows[:].bitcast(I32), 0)
         nc.vector.memset(tab_rows[:].bitcast(I32), 0)
         nc.vector.memset(warm[:, 0:1], 0.0)
+        nc.gpsimd.memset(w8_plane[:].bitcast(I32), 0)
+        nc.sync.dma_start(list2[:], offs2)
+        for r in range(4):
+            queue = nc.sync if r < 2 else nc.scalar
+            queue.dma_start(tab2_rows[:].bitcast(I32)[r:P:32, :], tab2_scales.bitcast(I32)[0, r:16:4, :])
+        for r in range(4):
+            nc.scalar.dma_start(w4_rows[:].bitcast(I32)[r:P:32, :], w4_scales.bitcast(I32)[0, r:16:4, :])
         nc.scalar.activation(warm[:, 1:2], warm[:, 0:1], ACT.Sigmoid)
-        nc.vector.memset(tab2_rows[:].bitcast(I32), 0)
-        nc.vector.memset(weight_rows[:].bitcast(I32), 0)
 
         def load_w1(g, a, tag):
             raw = keep.tile([P, PACK, PASS], F32, name="w1_raw", tag=tag, align_bytes=64)
@@ -62,34 +70,20 @@ def tile_list_tissue_share_scores_kernel(
             nc.sync.dma_start(table[:], words.rearrange("p t i -> p (t i)").bitcast(I32))
             return table
 
+        w4_raw = held([P, 2 * H], U8, "w4_raw")
+        nc.sync.dma_start(w4_raw[:].bitcast(I32), w4_words.bitcast(I32)[0])
+        w1_raw = {}
+        w1_raw[0, 0] = load_w1(0, 0, "raw00")
         nc.sync.dma_start(lists[:], offs)
         for i in range(2):
             nc.sync.dma_start(
                 tab_rows[:].bitcast(I32)[i:P:PLANE_ROW, :],
                 tab_scales.bitcast(I32)[:, i:16:2, :].rearrange("a g t -> g a t"),
             )
-        w1_raw = {}
-        w1_raw[0, 0] = load_w1(0, 0, "raw00")
-        nc.sync.dma_start(list2[:], offs2)
-        for r in range(4):
-            nc.sync.dma_start(tab2_rows[:].bitcast(I32)[r:P:32, :], tab2_scales.bitcast(I32)[0, r:16:4, :])
-        w4_raw = held([P, 2 * H], U8, "w4_raw")
-        nc.sync.dma_start(w4_raw[:].bitcast(I32), w4_words.bitcast(I32)[0])
         w1_raw[0, 1] = load_w1(0, 1, "raw01")
-        for r in range(4):
-            nc.sync.dma_start(weight_rows[:].bitcast(I32)[r:P:32, :], w4_scales.bitcast(I32)[0, r:16:4, :])
         tab2 = load_words(tab2_words[0], "tab2")
         tab = [load_words(tab_words[a], "tab%d" % a) for a in range(PASSES)]
 
-        v_rows = held([P, S], U8, "v_rows")
-        nc.vector.tensor_copy(v_rows[:], tab_rows[:].indirect(lists[:]))
-        v_plane = held([P, S], U8, "v_plane")
-        nc.vector.tensor_copy(v_plane[:].bitcast(I32), v_rows[:].bitcast(I32))
-        for i in range(2):
-            nc.sync.dma_start(
-                v_plane[:].bitcast(I32)[2 + i : P - 16 + 2 : PLANE_ROW, :],
-                v_rows[:].bitcast(I32)[16 + i : P : PLANE_ROW, :],
-            )
         v2_plane = held([P, S], U8, "v2_plane")
         nc.vector.tensor_copy(v2_plane[:], tab2_rows[:].indirect(list2[:]))
         w4 = held([P, 2 * H], U8, "w4")
@@ -100,27 +94,37 @@ def tile_list_tissue_share_scores_kernel(
         w4_plane = held([P, H], U8, "w4_plane")
         nc.vector.tensor_copy(
             w4_plane[:].rearrange("p (g t m) -> p g t m", g=GROUPS, t=PACK),
-            weight_rows[:].rearrange("p (g m t) -> p g t m", g=GROUPS, t=PACK),
+            w4_rows[:].rearrange("p (g m t) -> p g t m", g=GROUPS, t=PACK),
         )
 
         def gather_words(table, offsets, half, name):
-            picked = held([P, JW], U32, name)
+            picked = keep.tile([P, JW], U32, name="picked", tag=name, align_bytes=64)
             part = offsets[:, half * (JW // 16) : (half + 1) * (JW // 16)]
             nc.vector.tensor_copy(picked[:], table[:].bitcast(U32).indirect(part))
             return picked
 
-        v2 = [gather_words(tab2, list2, half, "v2_%d" % half) for half in range(HALVES)]
-        w1_raw[1, 0] = load_w1(1, 0, "raw10")
-        w1_raw[1, 1] = load_w1(1, 1, "raw11")
+        v_rows = held([P, S], U8, "v_rows")
+        nc.vector.tensor_copy(v_rows[:], tab_rows[:].indirect(lists[:]))
+        v_plane = held([P, S], U8, "v_plane")
         gains = held([P, GROUPS, PACK], F32, "gains")
-        nc.sync.dma_start(gains[:], gain.rearrange("(g p t) -> p g t", g=GROUPS, t=PACK))
-        w8 = keep.tile([P, GROUPS, N], I32, name="w8", tag="tab2", align_bytes=64)
-        nc.sync.dma_start(w8[:], w8_words.rearrange("g p c i -> p g (c i)").bitcast(I32))
-        for d in range(4):
-            nc.sync.dma_start(
-                weight_rows[:].bitcast(I32)[32 * d : 32 * d + 4 * GROUPS, 0 : N // 4],
-                w8_scales.bitcast(I32)[:, 4 * d : 4 * d + 4, :],
-            )
+        w8 = held([P, GROUPS, N], I32, "w8")
+
+        def place_scale_rows():
+            nc.vector.tensor_copy(v_plane[:].bitcast(I32), v_rows[:].bitcast(I32))
+            for i in range(2):
+                nc.sync.dma_start(
+                    v_plane[:].bitcast(I32)[2 + i : P - 16 + 2 : PLANE_ROW, :],
+                    v_rows[:].bitcast(I32)[16 + i : P : PLANE_ROW, :],
+                )
+            for a in range(PASSES):
+                w1_raw[1, a] = load_w1(1, a, "raw1%d" % a)
+            nc.sync.dma_start(gains[:], gain.rearrange("(g p t) -> p g t", g=GROUPS, t=PACK))
+            nc.sync.dma_start(w8[:], w8_words.rearrange("g p c i -> p g (c i)").bitcast(I32))
+            for d in range(4):
+                nc.sync.dma_start(
+                    w8_plane[:].bitcast(I32)[32 * d : 32 * d + 4 * GROUPS, :],
+                    w8_scales.bitcast(I32)[:, 4 * d : 4 * d + 4, :],
+                )
 
         def bank(number):
             return psum.tile([P, JW], F32, name="bank", tag="bank%d" % number)
@@ -137,8 +141,8 @@ def tile_list_tissue_share_scores_kernel(
                 nc.vector.tensor_copy(dst, src)
             w1_bf[g, a] = grouped
 
-        def quantize_w1(g, a):
-            w1_codes[g, a] = held([P, PASS], U32, "w1_codes%d%d" % (g, a))
+        def quantize_w1(g, a, tag):
+            w1_codes[g, a] = keep.tile([P, PASS], U32, name="w1_codes", tag=tag, align_bytes=64)
             w1_plane[g, a] = held([P, PASS], U8, "w1_plane%d%d" % (g, a))
             nc.vector.quantize_mx(out=w1_codes[g, a][:].bitcast(FP8X4), scales=w1_plane[g, a][:], in_=w1_bf[g, a][:])
 
@@ -177,66 +181,85 @@ def tile_list_tissue_share_scores_kernel(
             tissue[g, half, t] = ring.tile([P, JW], F32, name="tissue", bufs=12)
             nc.scalar.activation(tissue[g, half, t][:], acc[:], ACT.Sigmoid)
 
-        h_codes, h_plane = {}, {}
+        slots, woven, h_codes, h_plane = {}, {}, {}, {}
 
-        def make_h(g, half, tag):
-            slots = keep.tile([P, PACK, JW], BF16, name="slots", tag=tag, align_bytes=64)
-            for t in range(PACK):
-                nc.vector.scalar_tensor_tensor(
-                    slots[:, t, :], tissue[g, half, t][:], gains[:, g, t : t + 1], unlike[g, half, t][:], ALU.mult, ALU.mult
-                )
-            woven = ring.tile([P, PACK * JW], BF16, name="woven", align_bytes=64)
-            nc.vector.tensor_copy(
-                woven[:].rearrange("p (c i t) -> p c t i", i=4, t=PACK),
-                slots[:].rearrange("p t (c i) -> p c t i", i=4),
+        def multiply(block, t, tag):
+            g, first, width = block
+            half, cols = first // JW, slice(first % JW, first % JW + width)
+            if t == 0:
+                slots[block] = keep.tile([P, PACK, width], BF16, name="slots", tag=tag, align_bytes=64)
+            nc.vector.scalar_tensor_tensor(
+                slots[block][:, t, :],
+                tissue[g, half, t][:, cols],
+                gains[:, g, t : t + 1],
+                unlike[g, half, t][:, cols],
+                ALU.mult,
+                ALU.mult,
             )
-            h_codes[g, half] = held([P, JW], U32, "h_codes%d%d" % (g, half))
-            h_plane[g, half] = held([P, JW], U8, "h_plane%d%d" % (g, half))
-            nc.vector.quantize_mx(out=h_codes[g, half][:].bitcast(FP8X4), scales=h_plane[g, half][:], in_=woven[:])
 
-        def scores(half, first_bank, squares):
-            for n in range(N // P):
-                y = bank(first_bank + n)
-                for g in range(GROUPS):
-                    nc.tensor.matmul_mx(
-                        out=y[:],
-                        lhsT=w8[:, g, P * n : P * (n + 1)].bitcast(FP8X4),
-                        lhsT_scale=weight_rows[4 * g : P, P * n : P * (n + 1)],
-                        rhs=h_codes[g, half][:].bitcast(FP8X4),
-                        rhs_scale=h_plane[g, half][:],
-                        start=(g == 0),
-                        stop=(g == GROUPS - 1),
-                    )
-                size = ring.tile([P, JW], F32, name="size")
-                nc.scalar.activation(size[:], y[:], ACT.Abs)
-                root = ring.tile([P, JW], F32, name="root", bufs=4)
-                nc.scalar.activation(root[:], size[:], ACT.Abs_reciprocal_sqrt, bias=1.0)
-                part = ring.tile([P, JW], F32, name="part", bufs=4)
-                score = held([P, JW], F32, "score%d%d" % (half, n))
-                if n >= N // P - squares:
-                    nc.scalar.activation(part[:], root[:], ACT.Square)
-                    nc.vector.tensor_tensor(score[:], y[:], part[:], ALU.mult)
-                else:
-                    nc.vector.tensor_tensor(part[:], y[:], root[:], ALU.mult)
-                    nc.vector.tensor_tensor(score[:], part[:], root[:], ALU.mult)
-                nc.sync.dma_start(out[P * n : P * (n + 1), JW * half : JW * (half + 1)], score[:])
+        def weave(block):
+            woven[block] = ring.tile([P, PACK * block[2]], BF16, name="woven", align_bytes=64)
+            nc.vector.tensor_copy(
+                woven[block][:].rearrange("p (c i t) -> p c t i", i=4, t=PACK),
+                slots[block][:].rearrange("p t (c i) -> p c t i", i=4),
+            )
+
+        def quantize_h(block):
+            h_codes[block] = held([P, block[2]], U32, "h_codes%d_%d" % block[:2])
+            h_plane[block] = held([P, block[2]], U8, "h_plane%d_%d" % block[:2])
+            nc.vector.quantize_mx(out=h_codes[block][:].bitcast(FP8X4), scales=h_plane[block][:], in_=woven[block][:])
+
+        def last_pass(dst, n, block, cols):
+            g = block[0]
+            nc.tensor.matmul_mx(
+                out=dst,
+                lhsT=w8[:, g, P * n : P * (n + 1)].bitcast(FP8X4),
+                lhsT_scale=w8_plane[4 * g : P, P * n : P * (n + 1)],
+                rhs=h_codes[block][:, cols].bitcast(FP8X4),
+                rhs_scale=h_plane[block][:, cols],
+                start=(g == 0),
+                stop=(g == GROUPS - 1),
+            )
+
+        def roots(y, square):
+            size = ring.tile([P, JW], F32, name="size")
+            nc.scalar.activation(size[:], y[:], ACT.Abs)
+            root = ring.tile([P, JW], F32, name="root", bufs=4)
+            nc.scalar.activation(root[:], size[:], ACT.Abs_reciprocal_sqrt, bias=1.0)
+            part = ring.tile([P, JW], F32, name="part", bufs=8)
+            if square:
+                nc.scalar.activation(part[:], root[:], ACT.Square)
+            return y, root, part, square
+
+        def score(sums, dst):
+            y, root, part, square = sums
+            result = ring.tile([P, JW], F32, name="result", bufs=8)
+            if square:
+                nc.vector.tensor_tensor(result[:], y[:], part[:], ALU.mult)
+            else:
+                nc.vector.tensor_tensor(part[:], y[:], root[:], ALU.mult)
+                nc.vector.tensor_tensor(result[:], part[:], root[:], ALU.mult)
+            nc.sync.dma_start(dst, result[:].rearrange("p (n c) -> p n c", n=dst.shape[1]))
 
         for a in range(PASSES):
             round_w1(0, a, True)
-            quantize_w1(0, a)
+        quantize_w1(0, 0, "w1_codes00")
+        place_scale_rows()
+        v2 = [gather_words(tab2, list2, half, "v2_%d" % half) for half in range(HALVES)]
         for g, half in ((0, 0), (0, 1), (1, 0)):
             for t in range(PACK):
                 control_product(g, half, t)
-        for half in range(HALVES):
-            for a in range(PASSES):
+        quantize_w1(0, 1, "tab2")
+        for a in range(PASSES):
+            for half in range(HALVES):
                 v[a, half] = gather_words(tab[a], lists, half, "v%d%d" % (a, half))
         for half in range(HALVES):
             for t in range(PACK):
                 tissue_product(0, half, t)
         for a in range(PASSES):
             round_w1(1, a, False)
-            quantize_w1(1, a)
-        make_h(0, 0, "raw11")
+        quantize_w1(1, 0, "raw11")
+        quantize_w1(1, 1, "w1_codes11")
         for t in range(PACK):
             tissue_product(1, 0, t)
         for t in range(PACK):
@@ -244,8 +267,38 @@ def tile_list_tissue_share_scores_kernel(
         for t in range(PACK):
             tissue_product(1, 1, t)
         nc.scalar.activation(warm[:, 1:2], tissue[1, 1, PACK - 1][:, 0:1], ACT.Abs_reciprocal_sqrt, bias=1.0)
-        make_h(1, 0, "raw10")
-        scores(0, 4, 4)
-        make_h(0, 1, "raw10")
-        make_h(1, 1, "raw11")
-        scores(1, 0, 2)
+
+        quarter = JW // 2
+        blocks = ((0, 0, JW), (1, 0, JW), (0, JW, JW), (1, JW, quarter), (1, JW + quarter, quarter))
+        tags = ("w1_bf10", "raw10", "unlike102", "tab0", "tab1")
+        for step, block in enumerate(blocks):
+            multiply(block, 0, tags[step])
+            if step > 0:
+                weave(blocks[step - 1])
+            multiply(block, 1, tags[step])
+            if step > 0:
+                quantize_h(blocks[step - 1])
+            multiply(block, 2, tags[step])
+            multiply(block, 3, tags[step])
+        weave(blocks[-1])
+        quantize_h(blocks[-1])
+
+        by_row = out.rearrange("(n p) j -> p n j", p=P)
+        pending = []
+        first = [bank(4 + n) for n in range(N // P)]
+        for g in range(GROUPS):
+            for n in range(N // P):
+                last_pass(first[n][:], n, blocks[g], slice(0, JW))
+        for n in range(N // P):
+            pending.append((roots(first[n], True), by_row[:, n : n + 1, 0:JW]))
+        for q in range(2):
+            for pair in range(2):
+                y = bank(2 * q + pair)
+                for n in (2 * pair, 2 * pair + 1):
+                    dst = y[:, quarter * (n % 2) : quarter * (n % 2 + 1)]
+                    last_pass(dst, n, blocks[2], slice(quarter * q, quarter * (q + 1)))
+                    last_pass(dst, n, blocks[3 + q], slice(0, quarter))
+                cols = slice(JW + quarter * q, JW + quarter * (q + 1))
+                pending.append((roots(y, q == 1), by_row[:, 2 * pair : 2 * pair + 2, cols]))
+        for sums, dst in pending:
+            score(sums, dst)

@@ -38,52 +38,63 @@ def tile_list_tissue_share_scores_kernel(
         def held(shape, dtype, name):
             return keep.tile(shape, dtype, name=name, align_bytes=64)
 
+        def reused(shape, dtype, name, tag):
+            return keep.tile(shape, dtype, name=name, tag=tag, align_bytes=64)
+
         lists = keep.tile([P, S // 16], U16, name="lists")
         list2 = keep.tile([P, S // 16], U16, name="list2")
         tab2_rows = held([P, T], U8, "tab2_rows")
-        tab_rows = held([P, T], U8, "tab_rows")
-        w4_rows = keep.tile([P, H], U8, name="w4_rows", tag="w4_rows", align_bytes=64)
+        tab_rows = reused([P, T], U8, "tab_rows", "tab_rows")
+        w4_rows = reused([P, H], U8, "w4_rows", "w4_rows")
         w8_plane = held([P, N], U8, "w8_plane")
         warm = held([P, 2], F32, "warm")
 
-        nc.gpsimd.memset(tab2_rows[:].bitcast(I32), 0)
-        nc.vector.memset(w4_rows[:].bitcast(I32), 0)
-        nc.vector.memset(tab_rows[:].bitcast(I32), 0)
+        nc.gpsimd.memset(tab_rows[:].bitcast(I32), 0)
         nc.vector.memset(warm[:, 0:1], 0.0)
+        nc.vector.memset(tab2_rows[:].bitcast(I32), 0)
+        nc.vector.memset(w4_rows[:].bitcast(I32), 0)
         nc.gpsimd.memset(w8_plane[:].bitcast(I32), 0)
-        nc.sync.dma_start(list2[:], offs2)
-        for r in range(4):
-            queue = nc.sync if r < 2 else nc.scalar
-            queue.dma_start(tab2_rows[:].bitcast(I32)[r:P:32, :], tab2_scales.bitcast(I32)[0, r:16:4, :])
-        for r in range(4):
-            nc.scalar.dma_start(w4_rows[:].bitcast(I32)[r:P:32, :], w4_scales.bitcast(I32)[0, r:16:4, :])
         nc.scalar.activation(warm[:, 1:2], warm[:, 0:1], ACT.Sigmoid)
 
-        def load_w1(g, a, tag):
-            raw = keep.tile([P, PACK, PASS], F32, name="w1_raw", tag=tag, align_bytes=64)
+        def load_w1(g, a):
+            raw = reused([P, PACK, PASS], F32, "w1_raw", "raw%d%d" % (g, a))
             rows = w1[PASS * a : PASS * (a + 1), PASS * g : PASS * (g + 1)]
             nc.sync.dma_start(raw[:], rows.rearrange("(p j) c -> p j c", j=PACK))
             return raw
 
         def load_words(words, tag):
-            table = keep.tile([P, T], I32, name="table", tag=tag, align_bytes=64)
+            table = reused([P, T], I32, "table", tag)
             nc.sync.dma_start(table[:], words.rearrange("p t i -> p (t i)").bitcast(I32))
             return table
 
-        w4_raw = held([P, 2 * H], U8, "w4_raw")
-        nc.sync.dma_start(w4_raw[:].bitcast(I32), w4_words.bitcast(I32)[0])
+        def load_w4_scales(r):
+            nc.sync.dma_start(w4_rows[:].bitcast(I32)[r:P:32, :], w4_scales.bitcast(I32)[0, r:16:4, :])
+
         w1_raw = {}
-        w1_raw[0, 0] = load_w1(0, 0, "raw00")
         nc.sync.dma_start(lists[:], offs)
+        nc.sync.dma_start(list2[:], offs2)
         for i in range(2):
             nc.sync.dma_start(
                 tab_rows[:].bitcast(I32)[i:P:PLANE_ROW, :],
                 tab_scales.bitcast(I32)[:, i:16:2, :].rearrange("a g t -> g a t"),
             )
-        w1_raw[0, 1] = load_w1(0, 1, "raw01")
+        w1_raw[0, 0] = load_w1(0, 0)
+        for r in range(4):
+            nc.sync.dma_start(tab2_rows[:].bitcast(I32)[r:P:32, :], tab2_scales.bitcast(I32)[0, r:16:4, :])
+        w4_raw = held([P, 2 * H], U8, "w4_raw")
+        nc.sync.dma_start(w4_raw[:].bitcast(I32), w4_words.bitcast(I32)[0])
+        load_w4_scales(0)
+        w1_raw[0, 1] = load_w1(0, 1)
+        for r in range(1, 4):
+            load_w4_scales(r)
         tab2 = load_words(tab2_words[0], "tab2")
         tab = [load_words(tab_words[a], "tab%d" % a) for a in range(PASSES)]
+        w1_raw[1, 0] = load_w1(1, 0)
 
+        v_rows = held([P, S], U8, "v_rows")
+        nc.vector.tensor_copy(v_rows[:], tab_rows[:].indirect(lists[:]))
+        v_plane = held([P, S], U8, "v_plane")
+        nc.vector.tensor_copy(v_plane[:].bitcast(I32), v_rows[:].bitcast(I32))
         v2_plane = held([P, S], U8, "v2_plane")
         nc.vector.tensor_copy(v2_plane[:], tab2_rows[:].indirect(list2[:]))
         w4 = held([P, 2 * H], U8, "w4")
@@ -97,34 +108,28 @@ def tile_list_tissue_share_scores_kernel(
             w4_rows[:].rearrange("p (g m t) -> p g t m", g=GROUPS, t=PACK),
         )
 
-        def gather_words(table, offsets, half, name):
-            picked = keep.tile([P, JW], U32, name="picked", tag=name, align_bytes=64)
-            part = offsets[:, half * (JW // 16) : (half + 1) * (JW // 16)]
-            nc.vector.tensor_copy(picked[:], table[:].bitcast(U32).indirect(part))
-            return picked
-
-        v_rows = held([P, S], U8, "v_rows")
-        nc.vector.tensor_copy(v_rows[:], tab_rows[:].indirect(lists[:]))
-        v_plane = held([P, S], U8, "v_plane")
-        gains = held([P, GROUPS, PACK], F32, "gains")
-        w8 = held([P, GROUPS, N], I32, "w8")
-
-        def place_scale_rows():
-            nc.vector.tensor_copy(v_plane[:].bitcast(I32), v_rows[:].bitcast(I32))
+        v2 = []
+        for half in range(HALVES):
+            v2.append(held([P, JW], U32, "v2_%d" % half))
+            part = list2[:, half * (JW // 16) : (half + 1) * (JW // 16)]
+            nc.vector.tensor_copy(v2[half][:], tab2[:].bitcast(U32).indirect(part))
+        for a in range(PASSES):
             for i in range(2):
+                row = PLANE_ROW * a + i
                 nc.sync.dma_start(
-                    v_plane[:].bitcast(I32)[2 + i : P - 16 + 2 : PLANE_ROW, :],
-                    v_rows[:].bitcast(I32)[16 + i : P : PLANE_ROW, :],
+                    v_plane[:].bitcast(I32)[row + 2 : P : 32, :],
+                    v_rows[:].bitcast(I32)[row + 16 : P : 32, :],
                 )
-            for a in range(PASSES):
-                w1_raw[1, a] = load_w1(1, a, "raw1%d" % a)
-            nc.sync.dma_start(gains[:], gain.rearrange("(g p t) -> p g t", g=GROUPS, t=PACK))
-            nc.sync.dma_start(w8[:], w8_words.rearrange("g p c i -> p g (c i)").bitcast(I32))
-            for d in range(4):
-                nc.sync.dma_start(
-                    w8_plane[:].bitcast(I32)[32 * d : 32 * d + 4 * GROUPS, :],
-                    w8_scales.bitcast(I32)[:, 4 * d : 4 * d + 4, :],
-                )
+        w1_raw[1, 1] = load_w1(1, 1)
+        gains = held([P, GROUPS, PACK], F32, "gains")
+        nc.sync.dma_start(gains[:], gain.rearrange("(g p t) -> p g t", g=GROUPS, t=PACK))
+        w8 = held([P, GROUPS, N], I32, "w8")
+        nc.sync.dma_start(w8[:], w8_words.rearrange("g p c i -> p g (c i)").bitcast(I32))
+        for d in range(4):
+            nc.sync.dma_start(
+                w8_plane[:].bitcast(I32)[32 * d : 32 * d + 4 * GROUPS, :],
+                w8_scales.bitcast(I32)[:, 4 * d : 4 * d + 4, :],
+            )
 
         def bank(number):
             return psum.tile([P, JW], F32, name="bank", tag="bank%d" % number)
@@ -132,7 +137,7 @@ def tile_list_tissue_share_scores_kernel(
         w1_codes, w1_plane, w1_bf = {}, {}, {}
 
         def round_w1(g, a, on_scalar):
-            grouped = keep.tile([P, PACK * PASS], BF16, name="grouped", tag="w1_bf%d%d" % (g, a), align_bytes=64)
+            grouped = reused([P, PACK * PASS], BF16, "grouped", "w1_bf%d%d" % (g, a))
             dst = grouped[:].rearrange("p (t m j) -> p m j t", t=PACK, j=PACK)
             src = w1_raw[g, a][:].rearrange("p j (m t) -> p m j t", t=PACK)
             if on_scalar:
@@ -142,13 +147,15 @@ def tile_list_tissue_share_scores_kernel(
             w1_bf[g, a] = grouped
 
         def quantize_w1(g, a, tag):
-            w1_codes[g, a] = keep.tile([P, PASS], U32, name="w1_codes", tag=tag, align_bytes=64)
+            w1_codes[g, a] = reused([P, PASS], U32, "w1_codes", tag)
             w1_plane[g, a] = held([P, PASS], U8, "w1_plane%d%d" % (g, a))
             nc.vector.quantize_mx(out=w1_codes[g, a][:].bitcast(FP8X4), scales=w1_plane[g, a][:], in_=w1_bf[g, a][:])
 
-        unlike, tissue = {}, {}
+        unlike = [held([P, PACK, S], F32, "unlike%d" % g) for g in range(GROUPS)]
+        tissue = [held([P, PACK, S], F32, "tissue%d" % g) for g in range(GROUPS)]
 
         def control_product(g, half, t):
+            cols = slice(JW * half, JW * (half + 1))
             col = PASS * g + P * t
             b = bank(t)
             nc.tensor.matmul_mx(
@@ -156,49 +163,47 @@ def tile_list_tissue_share_scores_kernel(
                 lhsT=w4[:, 2 * col : 2 * (col + P)].bitcast(FP4X4),
                 lhsT_scale=w4_plane[:, col : col + P],
                 rhs=v2[half][:].bitcast(FP8X4),
-                rhs_scale=v2_plane[:, JW * half : JW * (half + 1)],
+                rhs_scale=v2_plane[:, cols],
                 start=True,
                 stop=True,
             )
-            tag = "unlike%d%d%d" % (g, half, t)
-            unlike[g, half, t] = keep.tile([P, JW], F32, name="unlike", tag=tag, align_bytes=64)
-            nc.scalar.activation(unlike[g, half, t][:], b[:], ACT.Sigmoid, scale=-1.0)
+            nc.scalar.activation(unlike[g][:, t, cols], b[:], ACT.Sigmoid, scale=-1.0)
 
         v = {}
 
+        def gather_tissue_words(a):
+            v[a] = held([P, S], U32, "v%d" % a)
+            nc.vector.tensor_copy(v[a][:], tab[a][:].bitcast(U32).indirect(lists[:]))
+
         def tissue_product(g, half, t):
+            cols = slice(JW * half, JW * (half + 1))
+            rows = slice(P * t, P * (t + 1))
             acc = bank(t)
             for a in range(PASSES):
                 nc.tensor.matmul_mx(
                     out=acc[:],
-                    lhsT=w1_codes[g, a][:, P * t : P * (t + 1)].bitcast(FP8X4),
-                    lhsT_scale=w1_plane[g, a][:, P * t : P * (t + 1)],
-                    rhs=v[a, half][:].bitcast(FP8X4),
-                    rhs_scale=v_plane[PLANE_ROW * a : P, JW * half : JW * (half + 1)],
+                    lhsT=w1_codes[g, a][:, rows].bitcast(FP8X4),
+                    lhsT_scale=w1_plane[g, a][:, rows],
+                    rhs=v[a][:, cols].bitcast(FP8X4),
+                    rhs_scale=v_plane[PLANE_ROW * a : P, cols],
                     start=(a == 0),
                     stop=(a == PASSES - 1),
                 )
-            tissue[g, half, t] = ring.tile([P, JW], F32, name="tissue", bufs=12)
-            nc.scalar.activation(tissue[g, half, t][:], acc[:], ACT.Sigmoid)
+            nc.scalar.activation(tissue[g][:, t, cols], acc[:], ACT.Sigmoid)
 
         slots, woven, h_codes, h_plane = {}, {}, {}, {}
 
         def multiply(block, t, tag):
             g, first, width = block
-            half, cols = first // JW, slice(first % JW, first % JW + width)
+            cols = slice(first, first + width)
             if t == 0:
-                slots[block] = keep.tile([P, PACK, width], BF16, name="slots", tag=tag, align_bytes=64)
+                slots[block] = reused([P, PACK, width], BF16, "slots", tag)
             nc.vector.scalar_tensor_tensor(
-                slots[block][:, t, :],
-                tissue[g, half, t][:, cols],
-                gains[:, g, t : t + 1],
-                unlike[g, half, t][:, cols],
-                ALU.mult,
-                ALU.mult,
+                slots[block][:, t, :], tissue[g][:, t, cols], gains[:, g, t : t + 1], unlike[g][:, t, cols], ALU.mult, ALU.mult
             )
 
-        def weave(block):
-            woven[block] = ring.tile([P, PACK * block[2]], BF16, name="woven", align_bytes=64)
+        def weave(block, tag):
+            woven[block] = reused([P, PACK * block[2]], BF16, "woven", tag)
             nc.vector.tensor_copy(
                 woven[block][:].rearrange("p (c i t) -> p c t i", i=4, t=PACK),
                 slots[block][:].rearrange("p t (c i) -> p c t i", i=4),
@@ -209,8 +214,9 @@ def tile_list_tissue_share_scores_kernel(
             h_plane[block] = held([P, block[2]], U8, "h_plane%d_%d" % block[:2])
             nc.vector.quantize_mx(out=h_codes[block][:].bitcast(FP8X4), scales=h_plane[block][:], in_=woven[block][:])
 
-        def last_pass(dst, n, block, cols):
+        def last_pass(dst, n, block, first, width):
             g = block[0]
+            cols = slice(first - block[1], first - block[1] + width)
             nc.tensor.matmul_mx(
                 out=dst,
                 lhsT=w8[:, g, P * n : P * (n + 1)].bitcast(FP8X4),
@@ -221,84 +227,84 @@ def tile_list_tissue_share_scores_kernel(
                 stop=(g == GROUPS - 1),
             )
 
-        def roots(y, square):
-            size = ring.tile([P, JW], F32, name="size")
-            nc.scalar.activation(size[:], y[:], ACT.Abs)
-            root = ring.tile([P, JW], F32, name="root", bufs=4)
-            nc.scalar.activation(root[:], size[:], ACT.Abs_reciprocal_sqrt, bias=1.0)
-            part = ring.tile([P, JW], F32, name="part", bufs=8)
-            if square:
-                nc.scalar.activation(part[:], root[:], ACT.Square)
-            return y, root, part, square
+        def inverse(pair, squared):
+            size = ring.tile([P, 2, JW], F32, name="size")
+            for e in range(2):
+                nc.scalar.activation(size[:, e, :], pair[e][:], ACT.Abs)
+            root = ring.tile([P, 2, JW], F32, name="root")
+            for e in range(2):
+                nc.scalar.activation(root[:, e, :], size[:, e, :], ACT.Abs_reciprocal_sqrt, bias=1.0)
+            part = ring.tile([P, 2, JW], F32, name="part", bufs=4)
+            for e in squared:
+                nc.scalar.activation(part[:, e, :], root[:, e, :], ACT.Square)
+            return root, part, squared
 
-        def score(sums, dst):
-            y, root, part, square = sums
-            result = ring.tile([P, JW], F32, name="result", bufs=8)
-            if square:
-                nc.vector.tensor_tensor(result[:], y[:], part[:], ALU.mult)
-            else:
-                nc.vector.tensor_tensor(part[:], y[:], root[:], ALU.mult)
-                nc.vector.tensor_tensor(result[:], part[:], root[:], ALU.mult)
-            nc.sync.dma_start(dst, result[:].rearrange("p (n c) -> p n c", n=dst.shape[1]))
+        def score(pair, factors, dst):
+            root, part, squared = factors
+            for e in range(2):
+                result = ring.tile([P, JW], F32, name="result", bufs=8)
+                if e in squared:
+                    nc.vector.tensor_tensor(result[:], pair[e][:], part[:, e, :], ALU.mult)
+                else:
+                    nc.vector.tensor_tensor(part[:, e, :], pair[e][:], root[:, e, :], ALU.mult)
+                    nc.vector.tensor_tensor(result[:], part[:, e, :], root[:, e, :], ALU.mult)
+                rows = dst.shape[1] // 2
+                nc.sync.dma_start(dst[:, rows * e : rows * (e + 1), :], result[:].rearrange("p (n c) -> p n c", n=rows))
 
         for a in range(PASSES):
             round_w1(0, a, True)
-        quantize_w1(0, 0, "w1_codes00")
-        place_scale_rows()
-        v2 = [gather_words(tab2, list2, half, "v2_%d" % half) for half in range(HALVES)]
-        for g, half in ((0, 0), (0, 1), (1, 0)):
+        quantize_w1(0, 0, "w4_rows")
+        quantize_w1(0, 1, "tab2")
+        for g, half in ((0, 0), (1, 0), (0, 1)):
             for t in range(PACK):
                 control_product(g, half, t)
-        quantize_w1(0, 1, "tab2")
         for a in range(PASSES):
-            for half in range(HALVES):
-                v[a, half] = gather_words(tab[a], lists, half, "v%d%d" % (a, half))
-        for half in range(HALVES):
-            for t in range(PACK):
-                tissue_product(0, half, t)
+            gather_tissue_words(a)
         for a in range(PASSES):
             round_w1(1, a, False)
         quantize_w1(1, 0, "raw11")
         quantize_w1(1, 1, "w1_codes11")
         for t in range(PACK):
-            tissue_product(1, 0, t)
+            tissue_product(0, 0, t)
         for t in range(PACK):
             control_product(1, 1, t)
-        for t in range(PACK):
-            tissue_product(1, 1, t)
-        nc.scalar.activation(warm[:, 1:2], tissue[1, 1, PACK - 1][:, 0:1], ACT.Abs_reciprocal_sqrt, bias=1.0)
+        for g, half in ((1, 0), (0, 1), (1, 1)):
+            for t in range(PACK):
+                tissue_product(g, half, t)
+        nc.scalar.activation(warm[:, 1:2], tissue[1][:, PACK - 1, S - 1 : S], ACT.Abs_reciprocal_sqrt, bias=1.0)
 
         quarter = JW // 2
         blocks = ((0, 0, JW), (1, 0, JW), (0, JW, JW), (1, JW, quarter), (1, JW + quarter, quarter))
-        tags = ("w1_bf10", "raw10", "unlike102", "tab0", "tab1")
+        slot_tags = ("w1_bf10", "w1_bf00", "w1_bf01", "tab0", "slots4")
+        woven_tags = ("raw10", "raw00", "raw01", "w1_bf11", "woven4")
         for step, block in enumerate(blocks):
-            multiply(block, 0, tags[step])
+            multiply(block, 0, slot_tags[step])
             if step > 0:
-                weave(blocks[step - 1])
-            multiply(block, 1, tags[step])
+                weave(blocks[step - 1], woven_tags[step - 1])
+            multiply(block, 1, slot_tags[step])
             if step > 0:
                 quantize_h(blocks[step - 1])
-            multiply(block, 2, tags[step])
-            multiply(block, 3, tags[step])
-        weave(blocks[-1])
+            multiply(block, 2, slot_tags[step])
+            multiply(block, 3, slot_tags[step])
+        weave(blocks[-1], woven_tags[-1])
         quantize_h(blocks[-1])
 
         by_row = out.rearrange("(n p) j -> p n j", p=P)
         pending = []
-        first = [bank(4 + n) for n in range(N // P)]
+        first_half = [bank(4 + n) for n in range(N // P)]
         for g in range(GROUPS):
             for n in range(N // P):
-                last_pass(first[n][:], n, blocks[g], slice(0, JW))
-        for n in range(N // P):
-            pending.append((roots(first[n], True), by_row[:, n : n + 1, 0:JW]))
-        for q in range(2):
-            for pair in range(2):
-                y = bank(2 * q + pair)
-                for n in (2 * pair, 2 * pair + 1):
-                    dst = y[:, quarter * (n % 2) : quarter * (n % 2 + 1)]
-                    last_pass(dst, n, blocks[2], slice(quarter * q, quarter * (q + 1)))
-                    last_pass(dst, n, blocks[3 + q], slice(0, quarter))
-                cols = slice(JW + quarter * q, JW + quarter * (q + 1))
-                pending.append((roots(y, q == 1), by_row[:, 2 * pair : 2 * pair + 2, cols]))
-        for sums, dst in pending:
-            score(sums, dst)
+                last_pass(first_half[n][:], n, blocks[g], 0, JW)
+        for u in range(2):
+            pair = first_half[2 * u : 2 * u + 2]
+            pending.append((pair, inverse(pair, (0, 1)), by_row[:, 2 * u : 2 * u + 2, 0:JW]))
+        for q, block in enumerate(blocks[3:]):
+            pair = [bank(2 * q + e) for e in range(2)]
+            first = block[1]
+            for n in range(N // P):
+                dst = pair[n // 2][:, quarter * (n % 2) : quarter * (n % 2 + 1)]
+                last_pass(dst, n, blocks[2], first, quarter)
+                last_pass(dst, n, block, first, quarter)
+            pending.append((pair, inverse(pair, ((1,), (0, 1))[q]), by_row[:, :, first : first + quarter]))
+        for pair, factors, dst in pending:
+            score(pair, factors, dst)

@@ -20,6 +20,7 @@ P = 128
 PACK = 4
 PASS = P * PACK
 JW = 512
+QW = JW // 2
 HALVES = S // JW
 GROUPS = H // PASS
 PASSES = K // PASS
@@ -108,11 +109,10 @@ def tile_list_tissue_share_scores_kernel(
             w4_rows[:].rearrange("p (g m t) -> p g t m", g=GROUPS, t=PACK),
         )
 
-        v2 = []
-        for half in range(HALVES):
-            v2.append(held([P, JW], U32, "v2_%d" % half))
-            part = list2[:, half * (JW // 16) : (half + 1) * (JW // 16)]
-            nc.vector.tensor_copy(v2[half][:], tab2[:].bitcast(U32).indirect(part))
+        v2 = held([P, S], U32, "v2")
+        for first, width in ((0, QW), (QW, QW), (JW, JW)):
+            part = list2[:, first // 16 : (first + width) // 16]
+            nc.vector.tensor_copy(v2[:, first : first + width], tab2[:].bitcast(U32).indirect(part))
         for a in range(PASSES):
             for i in range(2):
                 row = PLANE_ROW * a + i
@@ -151,8 +151,9 @@ def tile_list_tissue_share_scores_kernel(
             w1_plane[g, a] = held([P, PASS], U8, "w1_plane%d%d" % (g, a))
             nc.vector.quantize_mx(out=w1_codes[g, a][:].bitcast(FP8X4), scales=w1_plane[g, a][:], in_=w1_bf[g, a][:])
 
-        unlike = [held([P, PACK, S], F32, "unlike%d" % g) for g in range(GROUPS)]
-        tissue = [held([P, PACK, S], F32, "tissue%d" % g) for g in range(GROUPS)]
+        pieces = [(g, half) for g in range(GROUPS) for half in range(HALVES)]
+        unlike = {piece: held([P, PACK, JW], F32, "unlike%d%d" % piece) for piece in pieces}
+        tissue = {piece: held([P, PACK, JW], F32, "tissue%d%d" % piece) for piece in pieces}
 
         def control_product(g, half, t):
             cols = slice(JW * half, JW * (half + 1))
@@ -162,12 +163,28 @@ def tile_list_tissue_share_scores_kernel(
                 out=b[:],
                 lhsT=w4[:, 2 * col : 2 * (col + P)].bitcast(FP4X4),
                 lhsT_scale=w4_plane[:, col : col + P],
-                rhs=v2[half][:].bitcast(FP8X4),
+                rhs=v2[:, cols].bitcast(FP8X4),
                 rhs_scale=v2_plane[:, cols],
                 start=True,
                 stop=True,
             )
-            nc.scalar.activation(unlike[g][:, t, cols], b[:], ACT.Sigmoid, scale=-1.0)
+            nc.scalar.activation(unlike[g, half][:, t, :], b[:], ACT.Sigmoid, scale=-1.0)
+
+        def quarter_control_products(g, q, u):
+            b = bank(2 * g + u)
+            for e in range(2):
+                col = PASS * g + P * (2 * u + e)
+                nc.tensor.matmul_mx(
+                    out=b[:, QW * e : QW * (e + 1)],
+                    lhsT=w4[:, 2 * col : 2 * (col + P)].bitcast(FP4X4),
+                    lhsT_scale=w4_plane[:, col : col + P],
+                    rhs=v2[:, QW * q : QW * (q + 1)].bitcast(FP8X4),
+                    rhs_scale=v2_plane[:, QW * q : QW * (q + 1)],
+                    start=True,
+                    stop=True,
+                )
+            src = b[:].rearrange("p (e c) -> p e c", e=2)
+            nc.scalar.activation(unlike[g, 0][:, 2 * u : 2 * u + 2, QW * q : QW * (q + 1)], src, ACT.Sigmoid, scale=-1.0)
 
         v = {}
 
@@ -189,24 +206,24 @@ def tile_list_tissue_share_scores_kernel(
                     start=(a == 0),
                     stop=(a == PASSES - 1),
                 )
-            nc.scalar.activation(tissue[g][:, t, cols], acc[:], ACT.Sigmoid)
+            nc.scalar.activation(tissue[g, half][:, t, :], acc[:], ACT.Sigmoid)
 
-        slots, woven, h_codes, h_plane = {}, {}, {}, {}
+        woven, h_codes, h_plane = {}, {}, {}
 
-        def multiply(block, t, tag):
+        def apply_gain(g, half):
+            for t in range(PACK):
+                part = unlike[g, half][:, t, :]
+                nc.vector.tensor_scalar(part, part, gains[:, g, t : t + 1], None, ALU.mult)
+
+        def multiply(block, tag):
             g, first, width = block
-            cols = slice(first, first + width)
-            if t == 0:
-                slots[block] = reused([P, PACK, width], BF16, "slots", tag)
-            nc.vector.scalar_tensor_tensor(
-                slots[block][:, t, :], tissue[g][:, t, cols], gains[:, g, t : t + 1], unlike[g][:, t, cols], ALU.mult, ALU.mult
-            )
-
-        def weave(block, tag):
-            woven[block] = reused([P, PACK * block[2]], BF16, "woven", tag)
-            nc.vector.tensor_copy(
+            half, cols = first // JW, slice(first % JW, first % JW + width)
+            woven[block] = reused([P, PACK * width], BF16, "woven", tag)
+            nc.vector.tensor_tensor(
                 woven[block][:].rearrange("p (c i t) -> p c t i", i=4, t=PACK),
-                slots[block][:].rearrange("p t (c i) -> p c t i", i=4),
+                tissue[g, half][:, :, cols].rearrange("p t (c i) -> p c t i", i=4),
+                unlike[g, half][:, :, cols].rearrange("p t (c i) -> p c t i", i=4),
+                ALU.mult,
             )
 
         def quantize_h(block):
@@ -214,7 +231,7 @@ def tile_list_tissue_share_scores_kernel(
             h_plane[block] = held([P, block[2]], U8, "h_plane%d_%d" % block[:2])
             nc.vector.quantize_mx(out=h_codes[block][:].bitcast(FP8X4), scales=h_plane[block][:], in_=woven[block][:])
 
-        def last_pass(dst, n, block, first, width):
+        def last_pass(dst, n, block, first, width, start, stop):
             g = block[0]
             cols = slice(first - block[1], first - block[1] + width)
             nc.tensor.matmul_mx(
@@ -223,8 +240,8 @@ def tile_list_tissue_share_scores_kernel(
                 lhsT_scale=w8_plane[4 * g : P, P * n : P * (n + 1)],
                 rhs=h_codes[block][:, cols].bitcast(FP8X4),
                 rhs_scale=h_plane[block][:, cols],
-                start=(g == 0),
-                stop=(g == GROUPS - 1),
+                start=start,
+                stop=stop,
             )
 
         def inverse(pair, squared):
@@ -255,56 +272,58 @@ def tile_list_tissue_share_scores_kernel(
             round_w1(0, a, True)
         quantize_w1(0, 0, "w4_rows")
         quantize_w1(0, 1, "tab2")
-        for g, half in ((0, 0), (1, 0), (0, 1)):
+        for q in range(2):
+            for g in range(GROUPS):
+                for u in range(2):
+                    quarter_control_products(g, q, u)
+        for g in range(GROUPS):
             for t in range(PACK):
-                control_product(g, half, t)
+                control_product(g, 1, t)
         for a in range(PASSES):
             gather_tissue_words(a)
         for a in range(PASSES):
             round_w1(1, a, False)
         quantize_w1(1, 0, "raw11")
         quantize_w1(1, 1, "w1_codes11")
-        for t in range(PACK):
-            tissue_product(0, 0, t)
-        for t in range(PACK):
-            control_product(1, 1, t)
-        for g, half in ((1, 0), (0, 1), (1, 1)):
+        for g, half in ((0, 0), (1, 0), (0, 1), (1, 1)):
             for t in range(PACK):
                 tissue_product(g, half, t)
-        nc.scalar.activation(warm[:, 1:2], tissue[1][:, PACK - 1, S - 1 : S], ACT.Abs_reciprocal_sqrt, bias=1.0)
+        nc.scalar.activation(warm[:, 1:2], tissue[1, 1][:, PACK - 1, 0:1], ACT.Abs_reciprocal_sqrt, bias=1.0)
 
         quarter = JW // 2
         blocks = ((0, 0, JW), (1, 0, JW), (0, JW, JW), (1, JW, quarter), (1, JW + quarter, quarter))
-        slot_tags = ("w1_bf10", "w1_bf00", "w1_bf01", "tab0", "slots4")
-        woven_tags = ("raw10", "raw00", "raw01", "w1_bf11", "woven4")
-        for step, block in enumerate(blocks):
-            multiply(block, 0, slot_tags[step])
-            if step > 0:
-                weave(blocks[step - 1], woven_tags[step - 1])
-            multiply(block, 1, slot_tags[step])
-            if step > 0:
-                quantize_h(blocks[step - 1])
-            multiply(block, 2, slot_tags[step])
-            multiply(block, 3, slot_tags[step])
-        weave(blocks[-1], woven_tags[-1])
-        quantize_h(blocks[-1])
+        woven_tags = ("w1_bf10", "w1_bf11", "raw00", "raw01", "raw10")
+        apply_gain(0, 0)
+        apply_gain(1, 0)
+        multiply(blocks[0], woven_tags[0])
+        multiply(blocks[1], woven_tags[1])
+        quantize_h(blocks[0])
+        quantize_h(blocks[1])
+        apply_gain(0, 1)
+        multiply(blocks[2], woven_tags[2])
+        apply_gain(1, 1)
+        quantize_h(blocks[2])
+        multiply(blocks[3], woven_tags[3])
+        multiply(blocks[4], woven_tags[4])
+        quantize_h(blocks[3])
+        quantize_h(blocks[4])
 
         by_row = out.rearrange("(n p) j -> p n j", p=P)
         pending = []
         first_half = [bank(4 + n) for n in range(N // P)]
         for g in range(GROUPS):
             for n in range(N // P):
-                last_pass(first_half[n][:], n, blocks[g], 0, JW)
+                last_pass(first_half[n][:], n, blocks[g], 0, JW, g == 0, g == 1)
         for u in range(2):
             pair = first_half[2 * u : 2 * u + 2]
-            pending.append((pair, inverse(pair, (0, 1)), by_row[:, 2 * u : 2 * u + 2, 0:JW]))
+            pending.append((pair, inverse(pair, ((0, 1), (0,))[u]), by_row[:, 2 * u : 2 * u + 2, 0:JW]))
         for q, block in enumerate(blocks[3:]):
             pair = [bank(2 * q + e) for e in range(2)]
             first = block[1]
-            for n in range(N // P):
-                dst = pair[n // 2][:, quarter * (n % 2) : quarter * (n % 2 + 1)]
-                last_pass(dst, n, blocks[2], first, quarter)
-                last_pass(dst, n, block, first, quarter)
-            pending.append((pair, inverse(pair, ((1,), (0, 1))[q]), by_row[:, :, first : first + quarter]))
+            for g, source in enumerate((blocks[2], block)):
+                for n in range(N // P):
+                    dst = pair[n // 2][:, quarter * (n % 2) : quarter * (n % 2 + 1)]
+                    last_pass(dst, n, source, first, quarter, (g, n % 2) == (0, 0), (g, n % 2) == (1, 1))
+            pending.append((pair, inverse(pair, ((), (0, 1))[q]), by_row[:, :, first : first + quarter]))
         for pair, factors, dst in pending:
             score(pair, factors, dst)

@@ -195,7 +195,7 @@ def tile_list_tissue_share_scores_kernel(
         def tissue_product(g, half, t):
             cols = slice(JW * half, JW * (half + 1))
             rows = slice(P * t, P * (t + 1))
-            acc = bank(t)
+            acc = bank(t + 4 * (g == half))
             for a in range(PASSES):
                 nc.tensor.matmul_mx(
                     out=acc[:],
@@ -310,7 +310,7 @@ def tile_list_tissue_share_scores_kernel(
 
         by_row = out.rearrange("(n p) j -> p n j", p=P)
         pending = []
-        first_half = [bank(4 + n) for n in range(N // P)]
+        first_half = [bank(n) for n in range(N // P)]
         for g in range(GROUPS):
             for n in range(N // P):
                 last_pass(first_half[n][:], n, blocks[g], 0, JW, g == 0, g == 1)
@@ -318,7 +318,7 @@ def tile_list_tissue_share_scores_kernel(
             pair = first_half[2 * u : 2 * u + 2]
             pending.append((pair, inverse(pair, ((0, 1), (0,))[u]), by_row[:, 2 * u : 2 * u + 2, 0:JW]))
         for q, block in enumerate(blocks[3:]):
-            pair = [bank(2 * q + e) for e in range(2)]
+            pair = [bank(4 + 2 * q + e) for e in range(2)]
             first = block[1]
             for g, source in enumerate((blocks[2], block)):
                 for n in range(N // P):

@@ -82,13 +82,19 @@ def tile_list_tissue_share_scores_kernel(
         w1_raw[0, 0] = load_w1(0, 0)
         for r in range(4):
             nc.sync.dma_start(tab2_rows[:].bitcast(I32)[r:P:32, :], tab2_scales.bitcast(I32)[0, r:16:4, :])
-        w4_raw = held([P, 2 * H], U8, "w4_raw")
-        nc.sync.dma_start(w4_raw[:].bitcast(I32), w4_words.bitcast(I32)[0])
+        w4_raw = {}
+
+        def load_w4_words(g):
+            w4_raw[g] = held([P, 2 * PASS], U8, "w4_raw%d" % g)
+            nc.sync.dma_start(w4_raw[g][:].bitcast(I32), w4_words.bitcast(I32)[0, :, PASS // 2 * g : PASS // 2 * (g + 1)])
+
+        load_w4_words(0)
         load_w4_scales(0)
         w1_raw[0, 1] = load_w1(0, 1)
         for r in range(1, 4):
             load_w4_scales(r)
         tab2 = load_words(tab2_words[0], "tab2")
+        load_w4_words(1)
         tab = [load_words(tab_words[a], "tab%d" % a) for a in range(PASSES)]
         w1_raw[1, 0] = load_w1(1, 0)
 
@@ -98,11 +104,16 @@ def tile_list_tissue_share_scores_kernel(
         nc.vector.tensor_copy(v_plane[:].bitcast(I32), v_rows[:].bitcast(I32))
         v2_plane = held([P, S], U8, "v2_plane")
         nc.vector.tensor_copy(v2_plane[:], tab2_rows[:].indirect(list2[:]))
-        w4 = held([P, 2 * H], U8, "w4")
-        nc.vector.tensor_copy(
-            w4[:].bitcast(U16).rearrange("p (g t m) -> p g t m", g=GROUPS, t=PACK),
-            w4_raw[:].bitcast(U16).rearrange("p (g m t) -> p g t m", g=GROUPS, t=PACK),
-        )
+        w4 = {}
+
+        def deal_w4_words(g):
+            w4[g] = held([P, 2 * PASS], U8, "w4_%d" % g)
+            nc.vector.tensor_copy(
+                w4[g][:].bitcast(U16).rearrange("p (t m) -> p t m", t=PACK),
+                w4_raw[g][:].bitcast(U16).rearrange("p (m t) -> p t m", t=PACK),
+            )
+
+        deal_w4_words(0)
         w4_plane = held([P, H], U8, "w4_plane")
         nc.vector.tensor_copy(
             w4_plane[:].rearrange("p (g t m) -> p g t m", g=GROUPS, t=PACK),
@@ -113,6 +124,8 @@ def tile_list_tissue_share_scores_kernel(
         for first, width in ((0, QW), (QW, QW), (JW, JW)):
             part = list2[:, first // 16 : (first + width) // 16]
             nc.vector.tensor_copy(v2[:, first : first + width], tab2[:].bitcast(U32).indirect(part))
+            if first == QW:
+                deal_w4_words(1)
         for a in range(PASSES):
             for i in range(2):
                 row = PLANE_ROW * a + i
@@ -161,7 +174,7 @@ def tile_list_tissue_share_scores_kernel(
             b = bank(t)
             nc.tensor.matmul_mx(
                 out=b[:],
-                lhsT=w4[:, 2 * col : 2 * (col + P)].bitcast(FP4X4),
+                lhsT=w4[g][:, 2 * P * t : 2 * P * (t + 1)].bitcast(FP4X4),
                 lhsT_scale=w4_plane[:, col : col + P],
                 rhs=v2[:, cols].bitcast(FP8X4),
                 rhs_scale=v2_plane[:, cols],
@@ -171,12 +184,12 @@ def tile_list_tissue_share_scores_kernel(
             nc.scalar.activation(unlike[g, half][:, t, :], b[:], ACT.Sigmoid, scale=-1.0)
 
         def quarter_control_products(g, q, u):
-            b = bank(2 * g + u)
+            b = bank(2 * q + u)
             for e in range(2):
                 col = PASS * g + P * (2 * u + e)
                 nc.tensor.matmul_mx(
                     out=b[:, QW * e : QW * (e + 1)],
-                    lhsT=w4[:, 2 * col : 2 * (col + P)].bitcast(FP4X4),
+                    lhsT=w4[g][:, 2 * P * (2 * u + e) : 2 * P * (2 * u + e + 1)].bitcast(FP4X4),
                     lhsT_scale=w4_plane[:, col : col + P],
                     rhs=v2[:, QW * q : QW * (q + 1)].bitcast(FP8X4),
                     rhs_scale=v2_plane[:, QW * q : QW * (q + 1)],
@@ -244,7 +257,7 @@ def tile_list_tissue_share_scores_kernel(
                 stop=stop,
             )
 
-        def inverse(pair, squared):
+        def inverse(pair, squared, cuts):
             size = ring.tile([P, 2, JW], F32, name="size")
             for e in range(2):
                 nc.scalar.activation(size[:, e, :], pair[e][:], ACT.Abs)
@@ -253,32 +266,34 @@ def tile_list_tissue_share_scores_kernel(
                 nc.scalar.activation(root[:, e, :], size[:, e, :], ACT.Abs_reciprocal_sqrt, bias=1.0)
             part = ring.tile([P, 2, JW], F32, name="part", bufs=4)
             for e in squared:
-                nc.scalar.activation(part[:, e, :], root[:, e, :], ACT.Square)
-            return root, part, squared
+                for cols in cuts[e]:
+                    nc.scalar.activation(part[:, e, cols], root[:, e, cols], ACT.Square)
+            return root, part, squared, cuts
 
-        def score(pair, factors, dst):
-            root, part, squared = factors
-            for e in range(2):
-                result = ring.tile([P, JW], F32, name="result", bufs=8)
+        def score(pair, factors, dst, e):
+            root, part, squared, cuts = factors
+            result = ring.tile([P, JW], F32, name="result", bufs=8)
+            rows = dst.shape[1] // 2
+            for number, cols in enumerate(cuts[e]):
                 if e in squared:
-                    nc.vector.tensor_tensor(result[:], pair[e][:], part[:, e, :], ALU.mult)
+                    nc.vector.tensor_tensor(result[:, cols], pair[e][:, cols], part[:, e, cols], ALU.mult)
                 else:
-                    nc.vector.tensor_tensor(part[:, e, :], pair[e][:], root[:, e, :], ALU.mult)
-                    nc.vector.tensor_tensor(result[:], part[:, e, :], root[:, e, :], ALU.mult)
-                rows = dst.shape[1] // 2
-                nc.sync.dma_start(dst[:, rows * e : rows * (e + 1), :], result[:].rearrange("p (n c) -> p n c", n=rows))
+                    nc.vector.tensor_tensor(part[:, e, cols], pair[e][:, cols], root[:, e, cols], ALU.mult)
+                    nc.vector.tensor_tensor(result[:, cols], part[:, e, cols], root[:, e, cols], ALU.mult)
+                count = rows // len(cuts[e])
+                row = rows * e + count * number
+                nc.sync.dma_start(dst[:, row : row + count, :], result[:, cols].rearrange("p (n c) -> p n c", n=count))
 
         for a in range(PASSES):
             round_w1(0, a, True)
         quantize_w1(0, 0, "w4_rows")
         quantize_w1(0, 1, "tab2")
         for q in range(2):
-            for g in range(GROUPS):
-                for u in range(2):
-                    quarter_control_products(g, q, u)
-        for g in range(GROUPS):
+            for u in range(2):
+                quarter_control_products(0, q, u)
+        for g, half in ((1, 0), (0, 1), (1, 1)):
             for t in range(PACK):
-                control_product(g, 1, t)
+                control_product(g, half, t)
         for a in range(PASSES):
             gather_tissue_words(a)
         for a in range(PASSES):
@@ -291,24 +306,17 @@ def tile_list_tissue_share_scores_kernel(
         nc.scalar.activation(warm[:, 1:2], tissue[1, 1][:, PACK - 1, 0:1], ACT.Abs_reciprocal_sqrt, bias=1.0)
 
         quarter = JW // 2
-        blocks = ((0, 0, JW), (1, 0, JW), (0, JW, JW), (1, JW, quarter), (1, JW + quarter, quarter))
-        woven_tags = ("w1_bf10", "w1_bf11", "raw00", "raw01", "raw10")
+        blocks = [(0, 0, JW), (1, 0, JW)] + [(g, JW + quarter * q, quarter) for q in range(2) for g in range(GROUPS)]
+        woven_tags = ("w1_bf10", "w1_bf11", "raw00", "raw01", "raw10", "w1_bf00")
         apply_gain(0, 0)
         apply_gain(1, 0)
         multiply(blocks[0], woven_tags[0])
         multiply(blocks[1], woven_tags[1])
         quantize_h(blocks[0])
         quantize_h(blocks[1])
-        apply_gain(0, 1)
-        multiply(blocks[2], woven_tags[2])
-        apply_gain(1, 1)
-        quantize_h(blocks[2])
-        multiply(blocks[3], woven_tags[3])
-        multiply(blocks[4], woven_tags[4])
-        quantize_h(blocks[3])
-        quantize_h(blocks[4])
 
         by_row = out.rearrange("(n p) j -> p n j", p=P)
+        whole, halved = (slice(0, JW),), (slice(0, QW), slice(QW, JW))
         pending = []
         first_half = [bank(n) for n in range(N // P)]
         for g in range(GROUPS):
@@ -316,14 +324,24 @@ def tile_list_tissue_share_scores_kernel(
                 last_pass(first_half[n][:], n, blocks[g], 0, JW, g == 0, g == 1)
         for u in range(2):
             pair = first_half[2 * u : 2 * u + 2]
-            pending.append((pair, inverse(pair, ((0, 1), (0,))[u]), by_row[:, 2 * u : 2 * u + 2, 0:JW]))
-        for q, block in enumerate(blocks[3:]):
+            pending.append((pair, inverse(pair, (0, 1), (whole, whole)), by_row[:, 2 * u : 2 * u + 2, 0:JW]))
+
+        apply_gain(0, 1)
+        apply_gain(1, 1)
+        for q in range(2):
+            both = blocks[2 + 2 * q : 4 + 2 * q]
+            for g, block in enumerate(both):
+                multiply(block, woven_tags[2 + 2 * q + g])
+            for block in both:
+                quantize_h(block)
             pair = [bank(4 + 2 * q + e) for e in range(2)]
-            first = block[1]
-            for g, source in enumerate((blocks[2], block)):
+            first = both[0][1]
+            for g, source in enumerate(both):
                 for n in range(N // P):
                     dst = pair[n // 2][:, quarter * (n % 2) : quarter * (n % 2 + 1)]
                     last_pass(dst, n, source, first, quarter, (g, n % 2) == (0, 0), (g, n % 2) == (1, 1))
-            pending.append((pair, inverse(pair, ((), (0, 1))[q]), by_row[:, :, first : first + quarter]))
+            factors = inverse(pair, ((), (0, 1))[q], (whole, (whole, halved)[q]))
+            pending.append((pair, factors, by_row[:, :, first : first + quarter]))
         for pair, factors, dst in pending:
-            score(pair, factors, dst)
+            for e in range(2):
+                score(pair, factors, dst, e)

@@ -257,29 +257,30 @@ def tile_list_tissue_share_scores_kernel(
                 stop=stop,
             )
 
-        def inverse(pair, squared, cuts):
+        def inverse(pair, tags, cuts):
             size = ring.tile([P, 2, JW], F32, name="size")
             for e in range(2):
                 nc.scalar.activation(size[:, e, :], pair[e][:], ACT.Abs)
-            root = ring.tile([P, 2, JW], F32, name="root")
+            root = ring.tile([P, 2, JW], F32, name="root", bufs=3)
             for e in range(2):
                 nc.scalar.activation(root[:, e, :], size[:, e, :], ACT.Abs_reciprocal_sqrt, bias=1.0)
-            part = ring.tile([P, 2, JW], F32, name="part", bufs=4)
-            for e in squared:
-                for cols in cuts[e]:
-                    nc.scalar.activation(part[:, e, cols], root[:, e, cols], ACT.Square)
-            return root, part, squared, cuts
+            parts = []
+            for e in range(2):
+                if tags[e]:
+                    parts.append(reused([P, JW], F32, "part", tags[e]))
+                    nc.gpsimd.tensor_tensor(parts[e][:], root[:, e, :], root[:, e, :], ALU.mult)
+                else:
+                    parts.append(ring.tile([P, JW], F32, name="part", bufs=5))
+                    for cols in cuts[e]:
+                        nc.scalar.activation(parts[e][:, cols], root[:, e, cols], ACT.Square)
+            return parts, cuts
 
         def score(pair, factors, dst, e):
-            root, part, squared, cuts = factors
+            parts, cuts = factors
             result = ring.tile([P, JW], F32, name="result", bufs=8)
             rows = dst.shape[1] // 2
             for number, cols in enumerate(cuts[e]):
-                if e in squared:
-                    nc.vector.tensor_tensor(result[:, cols], pair[e][:, cols], part[:, e, cols], ALU.mult)
-                else:
-                    nc.vector.tensor_tensor(part[:, e, cols], pair[e][:, cols], root[:, e, cols], ALU.mult)
-                    nc.vector.tensor_tensor(result[:, cols], part[:, e, cols], root[:, e, cols], ALU.mult)
+                nc.vector.tensor_tensor(result[:, cols], pair[e][:, cols], parts[e][:, cols], ALU.mult)
                 count = rows // len(cuts[e])
                 row = rows * e + count * number
                 nc.sync.dma_start(dst[:, row : row + count, :], result[:, cols].rearrange("p (n c) -> p n c", n=count))
@@ -322,9 +323,6 @@ def tile_list_tissue_share_scores_kernel(
         for g in range(GROUPS):
             for n in range(N // P):
                 last_pass(first_half[n][:], n, blocks[g], 0, JW, g == 0, g == 1)
-        for u in range(2):
-            pair = first_half[2 * u : 2 * u + 2]
-            pending.append((pair, inverse(pair, (0, 1), (whole, whole)), by_row[:, 2 * u : 2 * u + 2, 0:JW]))
 
         apply_gain(0, 1)
         apply_gain(1, 1)
@@ -334,13 +332,18 @@ def tile_list_tissue_share_scores_kernel(
                 multiply(block, woven_tags[2 + 2 * q + g])
             for block in both:
                 quantize_h(block)
+        for u, tags in enumerate(((None, None), (None, woven_tags[-1]))):
+            pair = first_half[2 * u : 2 * u + 2]
+            pending.append((pair, inverse(pair, tags, (whole, whole)), by_row[:, 2 * u : 2 * u + 2, 0:JW]))
+        for q, tags in enumerate((("raw00", "raw01"), (None, None))):
+            both = blocks[2 + 2 * q : 4 + 2 * q]
             pair = [bank(4 + 2 * q + e) for e in range(2)]
             first = both[0][1]
             for g, source in enumerate(both):
                 for n in range(N // P):
                     dst = pair[n // 2][:, quarter * (n % 2) : quarter * (n % 2 + 1)]
                     last_pass(dst, n, source, first, quarter, (g, n % 2) == (0, 0), (g, n % 2) == (1, 1))
-            factors = inverse(pair, ((), (0, 1))[q], (whole, (whole, halved)[q]))
+            factors = inverse(pair, tags, (whole, (whole, halved)[q]))
             pending.append((pair, factors, by_row[:, :, first : first + quarter]))
         for pair, factors, dst in pending:
             for e in range(2):

@@ -1,6 +1,7 @@
 from contextlib import ExitStack
 
 import concourse.mybir as mybir
+from concourse.masks import make_identity
 
 K, K2, H, N, T, S = 1024, 512, 1024, 512, 2048, 1024
 FLOPS = 2 * S * (K * H + K2 * H + H * N)
@@ -46,7 +47,7 @@ def tile_list_tissue_share_scores_kernel(
         list2 = keep.tile([P, S // 16], U16, name="list2")
         tab2_rows = held([P, T], U8, "tab2_rows")
         tab_rows = reused([P, T], U8, "tab_rows", "tab_rows")
-        w4_rows = reused([P, H], U8, "w4_rows", "w4_rows")
+        w4_rows = held([P, H], U8, "w4_rows")
         w8_plane = held([P, N], U8, "w8_plane")
         warm = held([P, 2], F32, "warm")
 
@@ -55,6 +56,8 @@ def tile_list_tissue_share_scores_kernel(
         nc.vector.memset(tab2_rows[:].bitcast(I32), 0)
         nc.vector.memset(w4_rows[:].bitcast(I32), 0)
         nc.gpsimd.memset(w8_plane[:].bitcast(I32), 0)
+        identity = held([P, P], F32, "identity")
+        make_identity(nc, identity[:])
         nc.scalar.activation(warm[:, 1:2], warm[:, 0:1], ACT.Sigmoid)
 
         def load_w1(g, a):
@@ -85,7 +88,7 @@ def tile_list_tissue_share_scores_kernel(
         w4_raw = {}
 
         def load_w4_words(g):
-            w4_raw[g] = held([P, 2 * PASS], U8, "w4_raw%d" % g)
+            w4_raw[g] = reused([P, 2 * PASS], U8, "w4_raw", "w4_raw%d" % g)
             nc.sync.dma_start(w4_raw[g][:].bitcast(I32), w4_words.bitcast(I32)[0, :, PASS // 2 * g : PASS // 2 * (g + 1)])
 
         load_w4_words(0)
@@ -165,8 +168,29 @@ def tile_list_tissue_share_scores_kernel(
             nc.vector.quantize_mx(out=w1_codes[g, a][:].bitcast(FP8X4), scales=w1_plane[g, a][:], in_=w1_bf[g, a][:])
 
         pieces = [(g, half) for g in range(GROUPS) for half in range(HALVES)]
-        unlike = {piece: held([P, PACK, JW], F32, "unlike%d%d" % piece) for piece in pieces}
-        tissue = {piece: held([P, PACK, JW], F32, "tissue%d%d" % piece) for piece in pieces}
+        unlike = {piece: reused([P, PACK, JW], F32, "unlike", "unlike%d%d" % piece) for piece in pieces[:3]}
+        tissue = {piece: reused([P, PACK, JW], F32, "tissue", "tissue%d%d" % piece) for piece in pieces}
+        across, turned = {}, {}
+
+        def control_product_across(c):
+            cols = slice(JW + P * c, JW + P * (c + 1))
+            b = bank(c)
+            nc.tensor.matmul_mx(
+                out=b[:],
+                lhsT=v2[:, cols].bitcast(FP8X4),
+                lhsT_scale=v2_plane[:, cols],
+                rhs=w4_raw[1][:].bitcast(FP4X4),
+                rhs_scale=w4_rows[:, PASS:H],
+                start=True,
+                stop=True,
+            )
+            across[c] = held([P, PACK, P], F32, "across%d" % c)
+            nc.scalar.activation(across[c][:], b[:].rearrange("p (m t) -> p t m", t=PACK), ACT.Sigmoid, scale=-1.0)
+
+        def turn(c):
+            turned[c] = psum.tile([P, PACK, P], F32, name="turned", tag="bank%d" % (4 + c % 2))
+            for t in range(PACK):
+                nc.tensor.transpose(turned[c][:, t, :], across[c][:, t, :], identity[:])
 
         def control_product(g, half, t):
             cols = slice(JW * half, JW * (half + 1))
@@ -225,7 +249,7 @@ def tile_list_tissue_share_scores_kernel(
 
         def apply_gain(g, half):
             for t in range(PACK):
-                part = unlike[g, half][:, t, :]
+                part = (tissue if (g, half) == (1, 1) else unlike)[g, half][:, t, :]
                 nc.vector.tensor_scalar(part, part, gains[:, g, t : t + 1], None, ALU.mult)
 
         def multiply(block, tag):
@@ -238,6 +262,18 @@ def tile_list_tissue_share_scores_kernel(
                 unlike[g, half][:, :, cols].rearrange("p t (c i) -> p c t i", i=4),
                 ALU.mult,
             )
+
+        def multiply_turned(block, tag):
+            g, first, width = block
+            woven[block] = reused([P, PACK * width], BF16, "woven", tag)
+            for e in range(2):
+                c = (first - JW) // P + e
+                nc.vector.tensor_tensor(
+                    woven[block][:, PACK * P * e : PACK * P * (e + 1)].rearrange("p (c i t) -> p c t i", i=4, t=PACK),
+                    turned[c][:].rearrange("p t (c i) -> p c t i", i=4),
+                    tissue[1, 1][:, :, P * c : P * (c + 1)].rearrange("p t (c i) -> p c t i", i=4),
+                    ALU.mult,
+                )
 
         def quantize_h(block):
             h_codes[block] = held([P, block[2]], U32, "h_codes%d_%d" % block[:2])
@@ -275,9 +311,9 @@ def tile_list_tissue_share_scores_kernel(
                         nc.scalar.activation(parts[e][:, cols], root[:, e, cols], ACT.Square)
             return parts, cuts
 
-        def score(pair, factors, dst, e):
+        def score(pair, factors, dst, e, tag):
             parts, cuts = factors
-            result = ring.tile([P, JW], F32, name="result", bufs=8)
+            result = reused([P, JW], F32, "result", tag)
             rows = dst.shape[1] // 2
             for number, cols in enumerate(cuts[e]):
                 nc.vector.tensor_tensor(result[:, cols], pair[e][:, cols], parts[e][:, cols], ALU.mult)
@@ -287,14 +323,16 @@ def tile_list_tissue_share_scores_kernel(
 
         for a in range(PASSES):
             round_w1(0, a, True)
-        quantize_w1(0, 0, "w4_rows")
+        quantize_w1(0, 0, "w4_raw0")
         quantize_w1(0, 1, "tab2")
         for q in range(2):
             for u in range(2):
                 quarter_control_products(0, q, u)
-        for g, half in ((1, 0), (0, 1), (1, 1)):
+        for g, half in ((1, 0), (0, 1)):
             for t in range(PACK):
                 control_product(g, half, t)
+        for c in range(4):
+            control_product_across(c)
         for a in range(PASSES):
             gather_tissue_words(a)
         for a in range(PASSES):
@@ -324,27 +362,41 @@ def tile_list_tissue_share_scores_kernel(
             for n in range(N // P):
                 last_pass(first_half[n][:], n, blocks[g], 0, JW, g == 0, g == 1)
 
+        homes = ("tissue11", "tissue01", "unlike01", "tissue00", "tissue10", "unlike00", "unlike10", "tab0")
+
+        def quarter_passes(pair, source, step):
+            for n in range(N // P):
+                dst = pair[n // 2][:, quarter * (n % 2) : quarter * (n % 2 + 1)]
+                last_pass(dst, n, source, source[1], quarter, (step, n % 2) == (0, 0), (step, n % 2) == (1, 1))
+
+        for c in range(2):
+            turn(c)
         apply_gain(0, 1)
+        multiply(blocks[2], "raw00")
         apply_gain(1, 1)
-        for q in range(2):
-            both = blocks[2 + 2 * q : 4 + 2 * q]
-            for g, block in enumerate(both):
-                multiply(block, woven_tags[2 + 2 * q + g])
-            for block in both:
-                quantize_h(block)
-        for u, tags in enumerate(((None, None), (None, woven_tags[-1]))):
+        quantize_h(blocks[2])
+        third = [bank(6), bank(7)]
+        quarter_passes(third, blocks[2], 0)
+        multiply_turned(blocks[3], "raw01")
+        for c in range(2, 4):
+            turn(c)
+        quantize_h(blocks[3])
+        quarter_passes(third, blocks[3], 1)
+        multiply(blocks[4], "w1_bf00")
+        quantize_h(blocks[4])
+        multiply_turned(blocks[5], "raw10")
+        fourth = [bank(4), bank(5)]
+        quarter_passes(fourth, blocks[4], 0)
+        quantize_h(blocks[5])
+        quarter_passes(fourth, blocks[5], 1)
+        for u, tags in enumerate((("raw00", None), ("w1_bf00", "raw10"))):
             pair = first_half[2 * u : 2 * u + 2]
             pending.append((pair, inverse(pair, tags, (whole, whole)), by_row[:, 2 * u : 2 * u + 2, 0:JW]))
-        for q, tags in enumerate((("raw00", "raw01"), (None, None))):
-            both = blocks[2 + 2 * q : 4 + 2 * q]
-            pair = [bank(4 + 2 * q + e) for e in range(2)]
-            first = both[0][1]
-            for g, source in enumerate(both):
-                for n in range(N // P):
-                    dst = pair[n // 2][:, quarter * (n % 2) : quarter * (n % 2 + 1)]
-                    last_pass(dst, n, source, first, quarter, (g, n % 2) == (0, 0), (g, n % 2) == (1, 1))
+        for q, tags in enumerate((("w1_bf11", "w1_bf01"), (None, None))):
+            pair = (third, fourth)[q]
+            first = JW + quarter * q
             factors = inverse(pair, tags, (whole, (whole, halved)[q]))
             pending.append((pair, factors, by_row[:, :, first : first + quarter]))
-        for pair, factors, dst in pending:
+        for number, (pair, factors, dst) in enumerate(pending):
             for e in range(2):
-                score(pair, factors, dst, e)
+                score(pair, factors, dst, e, homes[2 * number + e])

@@ -392,11 +392,11 @@ def tile_list_tissue_share_scores_kernel(
         for u, tags in enumerate((("raw00", None), ("w1_bf00", "raw10"))):
             pair = first_half[2 * u : 2 * u + 2]
             pending.append((pair, inverse(pair, tags, (whole, whole)), by_row[:, 2 * u : 2 * u + 2, 0:JW]))
-        for q, tags in enumerate((("w1_bf11", "w1_bf01"), (None, None))):
+        for q, tags in enumerate((("w1_bf11", None), (None, None))):
             pair = (third, fourth)[q]
             first = JW + quarter * q
             factors = inverse(pair, tags, (whole, (whole, halved)[q]))
             pending.append((pair, factors, by_row[:, :, first : first + quarter]))
         for number, (pair, factors, dst) in enumerate(pending):
-            for e in range(2):
+            for e in (1, 0) if number == 2 else (0, 1):
                 score(pair, factors, dst, e, homes[2 * number + e])

@@ -392,11 +392,11 @@ def tile_list_tissue_share_scores_kernel(
         for u, tags in enumerate((("raw00", None), ("w1_bf00", "raw10"))):
             pair = first_half[2 * u : 2 * u + 2]
             pending.append((pair, inverse(pair, tags, (whole, whole)), by_row[:, 2 * u : 2 * u + 2, 0:JW]))
-        for q, tags in enumerate((("w1_bf11", None), (None, None))):
+        for q, tags in enumerate(((None, "w1_bf11"), (None, None))):
             pair = (third, fourth)[q]
             first = JW + quarter * q
             factors = inverse(pair, tags, (whole, (whole, halved)[q]))
             pending.append((pair, factors, by_row[:, :, first : first + quarter]))
         for number, (pair, factors, dst) in enumerate(pending):
-            for e in (1, 0) if number == 2 else (0, 1):
+            for e in range(2):
                 score(pair, factors, dst, e, homes[2 * number + e])

@@ -63,7 +63,10 @@ def tile_list_tissue_share_scores_kernel(
         def load_w1(g, a):
             raw = reused([P, PACK, PASS], F32, "w1_raw", "raw%d%d" % (g, a))
             rows = w1[PASS * a : PASS * (a + 1), PASS * g : PASS * (g + 1)]
-            nc.sync.dma_start(raw[:], rows.rearrange("(p j) c -> p j c", j=PACK))
+            by_row = rows.rearrange("(p j) c -> p j c", j=PACK)
+            if (g, a) == (0, 0):
+                return raw, by_row
+            nc.sync.dma_start(raw[:], by_row)
             return raw
 
         def load_words(words, tag):
@@ -75,6 +78,8 @@ def tile_list_tissue_share_scores_kernel(
             nc.sync.dma_start(w4_rows[:].bitcast(I32)[r:P:32, :], w4_scales.bitcast(I32)[0, r:16:4, :])
 
         w1_raw = {}
+        w1_raw[0, 0], first_rows = load_w1(0, 0)
+        nc.scalar.dma_start(w1_raw[0, 0][:, 0:2, :], first_rows[:, 0:2, :])
         nc.sync.dma_start(lists[:], offs)
         nc.sync.dma_start(list2[:], offs2)
         for i in range(2):
@@ -82,7 +87,7 @@ def tile_list_tissue_share_scores_kernel(
                 tab_rows[:].bitcast(I32)[i:P:PLANE_ROW, :],
                 tab_scales.bitcast(I32)[:, i:16:2, :].rearrange("a g t -> g a t"),
             )
-        w1_raw[0, 0] = load_w1(0, 0)
+        nc.sync.dma_start(w1_raw[0, 0][:, 2:4, :], first_rows[:, 2:4, :])
         for r in range(4):
             nc.sync.dma_start(tab2_rows[:].bitcast(I32)[r:P:32, :], tab2_scales.bitcast(I32)[0, r:16:4, :])
         w4_raw = {}
@@ -111,7 +116,7 @@ def tile_list_tissue_share_scores_kernel(
 
         def deal_w4_words(g):
             w4[g] = held([P, 2 * PASS], U8, "w4_%d" % g)
-            nc.vector.tensor_copy(
+            nc.scalar.copy(
                 w4[g][:].bitcast(U16).rearrange("p (t m) -> p t m", t=PACK),
                 w4_raw[g][:].bitcast(U16).rearrange("p (m t) -> p t m", t=PACK),
             )
@@ -124,7 +129,7 @@ def tile_list_tissue_share_scores_kernel(
         )
 
         v2 = held([P, S], U32, "v2")
-        for first, width in ((0, QW), (QW, QW), (JW, JW)):
+        for first, width in ((0, P), (P, P), (QW, QW), (JW, JW)):
             part = list2[:, first // 16 : (first + width) // 16]
             nc.vector.tensor_copy(v2[:, first : first + width], tab2[:].bitcast(U32).indirect(part))
             if first == QW:
@@ -207,21 +212,22 @@ def tile_list_tissue_share_scores_kernel(
             )
             nc.scalar.activation(unlike[g, half][:, t, :], b[:], ACT.Sigmoid, scale=-1.0)
 
-        def quarter_control_products(g, q, u):
-            b = bank(2 * q + u)
-            for e in range(2):
-                col = PASS * g + P * (2 * u + e)
+        def narrow_control_products(number, first, width, t0):
+            b = bank(number)
+            count = JW // width
+            for e in range(count):
+                t = t0 + e
                 nc.tensor.matmul_mx(
-                    out=b[:, QW * e : QW * (e + 1)],
-                    lhsT=w4[g][:, 2 * P * (2 * u + e) : 2 * P * (2 * u + e + 1)].bitcast(FP4X4),
-                    lhsT_scale=w4_plane[:, col : col + P],
-                    rhs=v2[:, QW * q : QW * (q + 1)].bitcast(FP8X4),
-                    rhs_scale=v2_plane[:, QW * q : QW * (q + 1)],
+                    out=b[:, width * e : width * (e + 1)],
+                    lhsT=w4[0][:, 2 * P * t : 2 * P * (t + 1)].bitcast(FP4X4),
+                    lhsT_scale=w4_plane[:, P * t : P * (t + 1)],
+                    rhs=v2[:, first : first + width].bitcast(FP8X4),
+                    rhs_scale=v2_plane[:, first : first + width],
                     start=True,
                     stop=True,
                 )
-            src = b[:].rearrange("p (e c) -> p e c", e=2)
-            nc.scalar.activation(unlike[g, 0][:, 2 * u : 2 * u + 2, QW * q : QW * (q + 1)], src, ACT.Sigmoid, scale=-1.0)
+            src = b[:].rearrange("p (e c) -> p e c", e=count)
+            nc.scalar.activation(unlike[0, 0][:, t0 : t0 + count, first : first + width], src, ACT.Sigmoid, scale=-1.0)
 
         v = {}
 
@@ -325,9 +331,8 @@ def tile_list_tissue_share_scores_kernel(
             round_w1(0, a, True)
         quantize_w1(0, 0, "w4_raw0")
         quantize_w1(0, 1, "tab2")
-        for q in range(2):
-            for u in range(2):
-                quarter_control_products(0, q, u)
+        for number, (first, width, t0) in enumerate(((0, P, 0), (P, P, 0), (QW, QW, 0), (QW, QW, 2))):
+            narrow_control_products(number, first, width, t0)
         for g, half in ((1, 0), (0, 1)):
             for t in range(PACK):
                 control_product(g, half, t)

@@ -26,6 +26,7 @@ HALVES = S // JW
 GROUPS = H // PASS
 PASSES = K // PASS
 PLANE_ROW = 8
+PLANE_START = 4
 
 
 def tile_list_tissue_share_scores_kernel(
@@ -84,7 +85,7 @@ def tile_list_tissue_share_scores_kernel(
         nc.sync.dma_start(list2[:], offs2)
         for i in range(2):
             nc.sync.dma_start(
-                tab_rows[:].bitcast(I32)[i:P:PLANE_ROW, :],
+                tab_rows[:].bitcast(I32)[PLANE_START + i : P : PLANE_ROW, :],
                 tab_scales.bitcast(I32)[:, i:16:2, :].rearrange("a g t -> g a t"),
             )
         nc.sync.dma_start(w1_raw[0, 0][:, 2:4, :], first_rows[:, 2:4, :])
@@ -136,7 +137,7 @@ def tile_list_tissue_share_scores_kernel(
                 deal_w4_words(1)
         for a in range(PASSES):
             for i in range(2):
-                row = PLANE_ROW * a + i
+                row = PLANE_START + PLANE_ROW * a + i
                 nc.sync.dma_start(
                     v_plane[:].bitcast(I32)[row + 2 : P : 32, :],
                     v_rows[:].bitcast(I32)[row + 16 : P : 32, :],
@@ -245,7 +246,7 @@ def tile_list_tissue_share_scores_kernel(
                     lhsT=w1_codes[g, a][:, rows].bitcast(FP8X4),
                     lhsT_scale=w1_plane[g, a][:, rows],
                     rhs=v[a][:, cols].bitcast(FP8X4),
-                    rhs_scale=v_plane[PLANE_ROW * a : P, cols],
+                    rhs_scale=v_plane[PLANE_START + PLANE_ROW * a : P, cols],
                     start=(a == 0),
                     stop=(a == PASSES - 1),
                 )

@@ -48,14 +48,18 @@ def tile_list_tissue_share_scores_kernel(
         list2 = keep.tile([P, S // 16], U16, name="list2")
         tab2_rows = held([P, T], U8, "tab2_rows")
         tab_rows = reused([P, T], U8, "tab_rows", "tab_rows")
-        w4_rows = held([P, H], U8, "w4_rows")
+        w4_rows = held([P, PASS], U8, "w4_rows")
+        w4_plane = held([P, H], U8, "w4_plane")
+        v2_plane = held([P, S], U8, "v2_plane")
         w8_plane = held([P, N], U8, "w8_plane")
         warm = held([P, 2], F32, "warm")
 
         nc.gpsimd.memset(tab_rows[:].bitcast(I32), 0)
         nc.vector.memset(warm[:, 0:1], 0.0)
-        nc.vector.memset(tab2_rows[:].bitcast(I32), 0)
         nc.vector.memset(w4_rows[:].bitcast(I32), 0)
+        nc.vector.memset(tab2_rows[:].bitcast(I32), 0)
+        nc.gpsimd.memset(w4_plane[:].bitcast(I32), 0)
+        nc.gpsimd.memset(v2_plane[:].bitcast(I32), 0)
         nc.gpsimd.memset(w8_plane[:].bitcast(I32), 0)
         identity = held([P, P], F32, "identity")
         make_identity(nc, identity[:])
@@ -75,22 +79,21 @@ def tile_list_tissue_share_scores_kernel(
             nc.sync.dma_start(table[:], words.rearrange("p t i -> p (t i)").bitcast(I32))
             return table
 
-        def load_w4_scales(r):
-            nc.sync.dma_start(w4_rows[:].bitcast(I32)[r:P:32, :], w4_scales.bitcast(I32)[0, r:16:4, :])
-
         w1_raw = {}
         w1_raw[0, 0], first_rows = load_w1(0, 0)
         nc.scalar.dma_start(w1_raw[0, 0][:, 0:2, :], first_rows[:, 0:2, :])
-        nc.sync.dma_start(lists[:], offs)
         nc.sync.dma_start(list2[:], offs2)
+        nc.sync.dma_start(lists[:], offs)
+        nc.sync.dma_start(
+            w4_rows[:].bitcast(I32)[0:P:4, :], w4_scales.bitcast(I32)[0].rearrange("q (g c) -> (q g) c", g=GROUPS)
+        )
+        nc.sync.dma_start(tab2_rows[:].bitcast(I32)[0:P:8, :], tab2_scales.bitcast(I32)[0])
         for i in range(2):
             nc.sync.dma_start(
                 tab_rows[:].bitcast(I32)[PLANE_START + i : P : PLANE_ROW, :],
                 tab_scales.bitcast(I32)[:, i:16:2, :].rearrange("a g t -> g a t"),
             )
         nc.sync.dma_start(w1_raw[0, 0][:, 2:4, :], first_rows[:, 2:4, :])
-        for r in range(4):
-            nc.sync.dma_start(tab2_rows[:].bitcast(I32)[r:P:32, :], tab2_scales.bitcast(I32)[0, r:16:4, :])
         w4_raw = {}
 
         def load_w4_words(g):
@@ -98,11 +101,22 @@ def tile_list_tissue_share_scores_kernel(
             nc.sync.dma_start(w4_raw[g][:].bitcast(I32), w4_words.bitcast(I32)[0, :, PASS // 2 * g : PASS // 2 * (g + 1)])
 
         load_w4_words(0)
-        load_w4_scales(0)
         w1_raw[0, 1] = load_w1(0, 1)
-        for r in range(1, 4):
-            load_w4_scales(r)
+        w4_dealt = held([P, PASS], U8, "w4_dealt")
+        nc.vector.tensor_copy(
+            w4_dealt[:].rearrange("p (t m) -> p t m", t=PACK), w4_rows[:].rearrange("p (m t) -> p t m", t=PACK)
+        )
+        for d in range(4):
+            nc.sync.dma_start(
+                w4_plane[:].bitcast(I32)[32 * d : 32 * d + 4, :], w4_dealt[:].bitcast(I32)[32 * d : 32 * (d + 1) : 4, :]
+            )
         tab2 = load_words(tab2_words[0], "tab2")
+        v2_rows = held([P, S], U8, "v2_rows")
+        nc.vector.tensor_copy(v2_rows[:], tab2_rows[:].indirect(list2[:]))
+        for d in range(4):
+            nc.sync.dma_start(
+                v2_plane[:].bitcast(I32)[32 * d : 32 * d + 4, :], v2_rows[:].bitcast(I32)[32 * d : 32 * (d + 1) : 8, :]
+            )
         load_w4_words(1)
         tab = [load_words(tab_words[a], "tab%d" % a) for a in range(PASSES)]
         w1_raw[1, 0] = load_w1(1, 0)
@@ -111,8 +125,6 @@ def tile_list_tissue_share_scores_kernel(
         nc.vector.tensor_copy(v_rows[:], tab_rows[:].indirect(lists[:]))
         v_plane = held([P, S], U8, "v_plane")
         nc.vector.tensor_copy(v_plane[:].bitcast(I32), v_rows[:].bitcast(I32))
-        v2_plane = held([P, S], U8, "v2_plane")
-        nc.vector.tensor_copy(v2_plane[:], tab2_rows[:].indirect(list2[:]))
         w4 = {}
 
         def deal_w4_words(g):
@@ -123,11 +135,6 @@ def tile_list_tissue_share_scores_kernel(
             )
 
         deal_w4_words(0)
-        w4_plane = held([P, H], U8, "w4_plane")
-        nc.vector.tensor_copy(
-            w4_plane[:].rearrange("p (g t m) -> p g t m", g=GROUPS, t=PACK),
-            w4_rows[:].rearrange("p (g m t) -> p g t m", g=GROUPS, t=PACK),
-        )
 
         v2 = held([P, S], U32, "v2")
         for first, width in ((0, P), (P, P), (QW, QW), (JW, JW)):
@@ -185,13 +192,13 @@ def tile_list_tissue_share_scores_kernel(
                 out=b[:],
                 lhsT=v2[:, cols].bitcast(FP8X4),
                 lhsT_scale=v2_plane[:, cols],
-                rhs=w4_raw[1][:].bitcast(FP4X4),
-                rhs_scale=w4_rows[:, PASS:H],
+                rhs=w4[1][:].bitcast(FP4X4),
+                rhs_scale=w4_plane[:, PASS:H],
                 start=True,
                 stop=True,
             )
             across[c] = held([P, PACK, P], F32, "across%d" % c)
-            nc.scalar.activation(across[c][:], b[:].rearrange("p (m t) -> p t m", t=PACK), ACT.Sigmoid, scale=-1.0)
+            nc.scalar.activation(across[c][:], b[:].rearrange("p (t m) -> p t m", t=PACK), ACT.Sigmoid, scale=-1.0)
 
         def turn(c):
             turned[c] = psum.tile([P, PACK, P], F32, name="turned", tag="bank%d" % (4 + c % 2))

@@ -25,7 +25,6 @@ QW = JW // 2
 HALVES = S // JW
 GROUPS = H // PASS
 PASSES = K // PASS
-PLANE_ROW = 8
 PLANE_START = 4
 
 
@@ -51,6 +50,7 @@ def tile_list_tissue_share_scores_kernel(
         w4_rows = held([P, PASS], U8, "w4_rows")
         w4_plane = held([P, H], U8, "w4_plane")
         v2_plane = held([P, S], U8, "v2_plane")
+        v_plane = held([P, PASSES * S], U8, "v_plane")
         w8_plane = held([P, N], U8, "w8_plane")
         warm = held([P, 2], F32, "warm")
 
@@ -58,9 +58,10 @@ def tile_list_tissue_share_scores_kernel(
         nc.vector.memset(warm[:, 0:1], 0.0)
         nc.vector.memset(w4_rows[:].bitcast(I32), 0)
         nc.vector.memset(tab2_rows[:].bitcast(I32), 0)
-        nc.gpsimd.memset(w4_plane[:].bitcast(I32), 0)
-        nc.gpsimd.memset(v2_plane[:].bitcast(I32), 0)
-        nc.gpsimd.memset(w8_plane[:].bitcast(I32), 0)
+        nc.vector.memset(w4_plane[:].bitcast(I32), 0)
+        nc.vector.memset(v2_plane[:].bitcast(I32), 0)
+        nc.vector.memset(v_plane[:].bitcast(I32), 0)
+        nc.vector.memset(w8_plane[:].bitcast(I32), 0)
         identity = held([P, P], F32, "identity")
         make_identity(nc, identity[:])
         nc.scalar.activation(warm[:, 1:2], warm[:, 0:1], ACT.Sigmoid)
@@ -88,11 +89,7 @@ def tile_list_tissue_share_scores_kernel(
             w4_rows[:].bitcast(I32)[0:P:4, :], w4_scales.bitcast(I32)[0].rearrange("q (g c) -> (q g) c", g=GROUPS)
         )
         nc.sync.dma_start(tab2_rows[:].bitcast(I32)[0:P:8, :], tab2_scales.bitcast(I32)[0])
-        for i in range(2):
-            nc.sync.dma_start(
-                tab_rows[:].bitcast(I32)[PLANE_START + i : P : PLANE_ROW, :],
-                tab_scales.bitcast(I32)[:, i:16:2, :].rearrange("a g t -> g a t"),
-            )
+        nc.sync.dma_start(tab_rows[:].bitcast(I32)[0:P:4, :], tab_scales.bitcast(I32).rearrange("a q t -> q a t"))
         nc.sync.dma_start(w1_raw[0, 0][:, 2:4, :], first_rows[:, 2:4, :])
         w4_raw = {}
 
@@ -123,8 +120,6 @@ def tile_list_tissue_share_scores_kernel(
 
         v_rows = held([P, S], U8, "v_rows")
         nc.vector.tensor_copy(v_rows[:], tab_rows[:].indirect(lists[:]))
-        v_plane = held([P, S], U8, "v_plane")
-        nc.vector.tensor_copy(v_plane[:].bitcast(I32), v_rows[:].bitcast(I32))
         w4 = {}
 
         def deal_w4_words(g):
@@ -142,13 +137,9 @@ def tile_list_tissue_share_scores_kernel(
             nc.vector.tensor_copy(v2[:, first : first + width], tab2[:].bitcast(U32).indirect(part))
             if first == QW:
                 deal_w4_words(1)
-        for a in range(PASSES):
-            for i in range(2):
-                row = PLANE_START + PLANE_ROW * a + i
-                nc.sync.dma_start(
-                    v_plane[:].bitcast(I32)[row + 2 : P : 32, :],
-                    v_rows[:].bitcast(I32)[row + 16 : P : 32, :],
-                )
+        for d in range(4):
+            row = 32 * d + PLANE_START
+            nc.sync.dma_start(v_plane[:].bitcast(I32)[row : row + 4, :], v_rows[:].bitcast(I32)[32 * d : 32 * (d + 1) : 4, :])
         w1_raw[1, 1] = load_w1(1, 1)
         gains = held([P, GROUPS, PACK], F32, "gains")
         nc.sync.dma_start(gains[:], gain.rearrange("(g p t) -> p g t", g=GROUPS, t=PACK))
@@ -253,7 +244,7 @@ def tile_list_tissue_share_scores_kernel(
                     lhsT=w1_codes[g, a][:, rows].bitcast(FP8X4),
                     lhsT_scale=w1_plane[g, a][:, rows],
                     rhs=v[a][:, cols].bitcast(FP8X4),
-                    rhs_scale=v_plane[PLANE_START + PLANE_ROW * a : P, cols],
+                    rhs_scale=v_plane[PLANE_START:P, S * a + JW * half : S * a + JW * (half + 1)],
                     start=(a == 0),
                     stop=(a == PASSES - 1),
                 )

@@ -35,7 +35,11 @@ def tile_list_tissue_share_scores_kernel(
     with ExitStack() as ctx:
         keep = ctx.enter_context(tc.tile_pool(name="keep", bufs=1))
         ring = ctx.enter_context(tc.tile_pool(name="ring", bufs=2))
+        laid = ctx.enter_context(tc.tile_pool(name="laid", bufs=1))
         psum = ctx.enter_context(tc.psum_pool(name="psum", bufs=1))
+
+        def placed(shape, dtype, name, offset):
+            return laid.tile(shape, dtype, name=name, align_bytes=64, offset=offset)
 
         def held(shape, dtype, name):
             return keep.tile(shape, dtype, name=name, align_bytes=64)
@@ -67,12 +71,21 @@ def tile_list_tissue_share_scores_kernel(
         nc.scalar.activation(warm[:, 1:2], warm[:, 0:1], ACT.Sigmoid)
 
         def load_w1(g, a):
-            raw = reused([P, PACK, PASS], F32, "w1_raw", "raw%d%d" % (g, a))
+            if (g, a) == (1, 1):
+                raw = placed([P, PACK, PASS], F32, "raw11", 0)
+            else:
+                raw = reused([P, PACK, PASS], F32, "w1_raw", "raw%d%d" % (g, a))
             rows = w1[PASS * a : PASS * (a + 1), PASS * g : PASS * (g + 1)]
             by_row = rows.rearrange("(p j) c -> p j c", j=PACK)
             if (g, a) == (0, 0):
                 return raw, by_row
             nc.sync.dma_start(raw[:], by_row)
+            return raw
+
+        def load_w1_half(u):
+            raw = reused([P, PACK, QW], F32, "w1_half", "half%d" % u)
+            rows = w1[PASS:K, QW * u : QW * (u + 1)]
+            nc.sync.dma_start(raw[:], rows.rearrange("(p j) c -> p j c", j=PACK))
             return raw
 
         def load_words(words, tag):
@@ -98,7 +111,7 @@ def tile_list_tissue_share_scores_kernel(
             nc.sync.dma_start(w4_raw[g][:].bitcast(I32), w4_words.bitcast(I32)[0, :, PASS // 2 * g : PASS // 2 * (g + 1)])
 
         load_w4_words(0)
-        w1_raw[0, 1] = load_w1(0, 1)
+        halves = [load_w1_half(0)]
         w4_dealt = held([P, PASS], U8, "w4_dealt")
         nc.vector.tensor_copy(
             w4_dealt[:].rearrange("p (t m) -> p t m", t=PACK), w4_rows[:].rearrange("p (m t) -> p t m", t=PACK)
@@ -114,8 +127,19 @@ def tile_list_tissue_share_scores_kernel(
             nc.sync.dma_start(
                 v2_plane[:].bitcast(I32)[32 * d : 32 * d + 4, :], v2_rows[:].bitcast(I32)[32 * d : 32 * (d + 1) : 8, :]
             )
+        halves.append(load_w1_half(1))
         load_w4_words(1)
         tab = [load_words(tab_words[a], "tab%d" % a) for a in range(PASSES)]
+        gains = {}
+
+        def load_gains(g, first, count):
+            part = held([P, count], F32, "gains%d%d" % (g, first))
+            by_row = gain[PASS * g : PASS * (g + 1)].rearrange("(p t) -> p t", t=PACK)
+            nc.sync.dma_start(part[:], by_row[:, first : first + count])
+            for t in range(count):
+                gains[g, first + t] = part[:, t : t + 1]
+
+        load_gains(0, 0, 3)
         w1_raw[1, 0] = load_w1(1, 0)
 
         v_rows = held([P, S], U8, "v_rows")
@@ -141,8 +165,8 @@ def tile_list_tissue_share_scores_kernel(
             row = 32 * d + PLANE_START
             nc.sync.dma_start(v_plane[:].bitcast(I32)[row : row + 4, :], v_rows[:].bitcast(I32)[32 * d : 32 * (d + 1) : 4, :])
         w1_raw[1, 1] = load_w1(1, 1)
-        gains = held([P, GROUPS, PACK], F32, "gains")
-        nc.sync.dma_start(gains[:], gain.rearrange("(g p t) -> p g t", g=GROUPS, t=PACK))
+        load_gains(0, 3, 1)
+        load_gains(1, 0, PACK)
         w8 = held([P, GROUPS, N], I32, "w8")
         nc.sync.dma_start(w8[:], w8_words.rearrange("g p c i -> p g (c i)").bitcast(I32))
         for d in range(4):
@@ -167,7 +191,7 @@ def tile_list_tissue_share_scores_kernel(
             w1_bf[g, a] = grouped
 
         def quantize_w1(g, a, tag):
-            w1_codes[g, a] = reused([P, PASS], U32, "w1_codes", tag)
+            w1_codes[g, a] = reused([P, PASS], U32, "w1_codes", tag) if tag else placed([P, PASS], U32, "w1_codes10", 0)
             w1_plane[g, a] = held([P, PASS], U8, "w1_plane%d%d" % (g, a))
             nc.vector.quantize_mx(out=w1_codes[g, a][:].bitcast(FP8X4), scales=w1_plane[g, a][:], in_=w1_bf[g, a][:])
 
@@ -192,7 +216,7 @@ def tile_list_tissue_share_scores_kernel(
             nc.scalar.activation(across[c][:], b[:].rearrange("p (t m) -> p t m", t=PACK), ACT.Sigmoid, scale=-1.0)
 
         def turn(c):
-            turned[c] = psum.tile([P, PACK, P], F32, name="turned", tag="bank%d" % (4 + c % 2))
+            turned[c] = psum.tile([P, PACK, P], F32, name="turned", tag="bank%d" % (6 + c % 2))
             for t in range(PACK):
                 nc.tensor.transpose(turned[c][:, t, :], across[c][:, t, :], identity[:])
 
@@ -234,10 +258,10 @@ def tile_list_tissue_share_scores_kernel(
             v[a] = held([P, S], U32, "v%d" % a)
             nc.vector.tensor_copy(v[a][:], tab[a][:].bitcast(U32).indirect(lists[:]))
 
-        def tissue_product(g, half, t):
+        def tissue_product(g, half, t, number):
             cols = slice(JW * half, JW * (half + 1))
             rows = slice(P * t, P * (t + 1))
-            acc = bank(t + 4 * (g == half))
+            acc = bank(number)
             for a in range(PASSES):
                 nc.tensor.matmul_mx(
                     out=acc[:],
@@ -252,10 +276,10 @@ def tile_list_tissue_share_scores_kernel(
 
         woven, h_codes, h_plane = {}, {}, {}
 
-        def apply_gain(g, half):
-            for t in range(PACK):
-                part = (tissue if (g, half) == (1, 1) else unlike)[g, half][:, t, :]
-                nc.vector.tensor_scalar(part, part, gains[:, g, t : t + 1], None, ALU.mult)
+        def apply_gain(g, half, rows=range(PACK), dst=None):
+            src = (tissue if (g, half) == (1, 1) else unlike)[g, half]
+            for t in rows:
+                nc.vector.tensor_scalar((dst or src)[:, t, :], src[:, t, :], gains[g, t], None, ALU.mult)
 
         def multiply(block, tag):
             g, first, width = block
@@ -326,8 +350,11 @@ def tile_list_tissue_share_scores_kernel(
                 row = rows * e + count * number
                 nc.sync.dma_start(dst[:, row : row + count, :], result[:, cols].rearrange("p (n c) -> p n c", n=count))
 
-        for a in range(PASSES):
-            round_w1(0, a, True)
+        round_w1(0, 0, True)
+        w1_bf[0, 1] = held([P, PACK * PASS], BF16, "w1_bf01")
+        for u, copy in enumerate((nc.scalar.copy, nc.vector.tensor_copy)):
+            dst = w1_bf[0, 1][:].rearrange("p (t m j) -> p m j t", t=PACK, j=PACK)[:, 64 * u : 64 * (u + 1)]
+            copy(dst, halves[u][:].rearrange("p j (m t) -> p m j t", t=PACK))
         quantize_w1(0, 0, "w4_raw0")
         quantize_w1(0, 1, "tab2")
         for number, (first, width, t0) in enumerate(((0, P, 0), (P, P, 0), (QW, QW, 0), (QW, QW, 2))):
@@ -337,31 +364,43 @@ def tile_list_tissue_share_scores_kernel(
                 control_product(g, half, t)
         for c in range(4):
             control_product_across(c)
+        nc.scalar.activation(unlike[0, 0][:, 2, :], unlike[0, 0][:, 2, :], ACT.Copy, scale=gains[0, 2])
         for a in range(PASSES):
             gather_tissue_words(a)
-        for a in range(PASSES):
-            round_w1(1, a, False)
-        quantize_w1(1, 0, "raw11")
+        round_w1(1, 0, False)
+        apply_gain(0, 0, (0, 1))
+        round_w1(1, 1, False)
+        quantize_w1(1, 0, None)
         quantize_w1(1, 1, "w1_codes11")
-        for g, half in ((0, 0), (1, 0), (0, 1), (1, 1)):
-            for t in range(PACK):
-                tissue_product(g, half, t)
+        for t in range(PACK):
+            tissue_product(0, 0, t, 4 + t)
+        for t in range(2):
+            tissue_product(0, 1, t, t)
+        later = [(1, 0, t) for t in range(PACK)] + [(0, 1, 2), (0, 1, 3)] + [(1, 1, t) for t in range(PACK)]
+        for number, (g, half, t) in enumerate(later):
+            tissue_product(g, half, t, (2, 3, 6, 7)[number % 4])
         nc.scalar.activation(warm[:, 1:2], tissue[1, 1][:, PACK - 1, 0:1], ACT.Abs_reciprocal_sqrt, bias=1.0)
 
         quarter = JW // 2
         blocks = [(0, 0, JW), (1, 0, JW)] + [(g, JW + quarter * q, quarter) for q in range(2) for g in range(GROUPS)]
-        woven_tags = ("w1_bf10", "w1_bf11", "raw00", "raw01", "raw10", "w1_bf00")
-        apply_gain(0, 0)
+        woven_tags = ("w1_bf10", "w1_bf11")
+        gained = placed([P, PACK, JW], F32, "gained01", 4 * PASS)
+        apply_gain(0, 0, (3,))
         apply_gain(1, 0)
         multiply(blocks[0], woven_tags[0])
-        multiply(blocks[1], woven_tags[1])
+        apply_gain(0, 1, (0,), gained)
         quantize_h(blocks[0])
+        apply_gain(0, 1, (1,), gained)
+        multiply(blocks[1], woven_tags[1])
+        apply_gain(0, 1, (2,), gained)
         quantize_h(blocks[1])
+        apply_gain(0, 1, (3,), gained)
+        unlike[0, 1] = gained
 
         by_row = out.rearrange("(n p) j -> p n j", p=P)
         whole, halved = (slice(0, JW),), (slice(0, QW), slice(QW, JW))
         pending = []
-        first_half = [bank(n) for n in range(N // P)]
+        first_half = [bank(n) for n in (0, 1, 4, 5)]
         for g in range(GROUPS):
             for n in range(N // P):
                 last_pass(first_half[n][:], n, blocks[g], 0, JW, g == 0, g == 1)
@@ -375,11 +414,10 @@ def tile_list_tissue_share_scores_kernel(
 
         for c in range(2):
             turn(c)
-        apply_gain(0, 1)
         multiply(blocks[2], "raw00")
         apply_gain(1, 1)
         quantize_h(blocks[2])
-        third = [bank(6), bank(7)]
+        third = [bank(2), bank(3)]
         quarter_passes(third, blocks[2], 0)
         multiply_turned(blocks[3], "raw01")
         for c in range(2, 4):
@@ -389,7 +427,7 @@ def tile_list_tissue_share_scores_kernel(
         multiply(blocks[4], "w1_bf00")
         quantize_h(blocks[4])
         multiply_turned(blocks[5], "raw10")
-        fourth = [bank(4), bank(5)]
+        fourth = [bank(6), bank(7)]
         quarter_passes(fourth, blocks[4], 0)
         quantize_h(blocks[5])
         quarter_passes(fourth, blocks[5], 1)

@@ -58,16 +58,17 @@ def tile_list_tissue_share_scores_kernel(
         w8_plane = held([P, N], U8, "w8_plane")
         warm = held([P, 2], F32, "warm")
 
-        nc.gpsimd.memset(tab_rows[:].bitcast(I32), 0)
+        nc.gpsimd.memset(w4_rows[:].bitcast(I32), 0)
+        nc.gpsimd.memset(tab2_rows[:].bitcast(I32), 0)
         nc.vector.memset(warm[:, 0:1], 0.0)
-        nc.vector.memset(w4_rows[:].bitcast(I32), 0)
-        nc.vector.memset(tab2_rows[:].bitcast(I32), 0)
+        nc.vector.memset(tab_rows[:].bitcast(I32), 0)
         nc.vector.memset(w4_plane[:].bitcast(I32), 0)
         nc.vector.memset(v2_plane[:].bitcast(I32), 0)
         nc.vector.memset(v_plane[:].bitcast(I32), 0)
         nc.vector.memset(w8_plane[:].bitcast(I32), 0)
         identity = held([P, P], F32, "identity")
-        make_identity(nc, identity[:])
+        nc.vector.memset(identity[:], 0.0)
+        make_identity(nc, identity[:], nomemset=True)
         nc.scalar.activation(warm[:, 1:2], warm[:, 0:1], ACT.Sigmoid)
 
         def load_w1(g, a):
@@ -116,17 +117,15 @@ def tile_list_tissue_share_scores_kernel(
         nc.vector.tensor_copy(
             w4_dealt[:].rearrange("p (t m) -> p t m", t=PACK), w4_rows[:].rearrange("p (m t) -> p t m", t=PACK)
         )
-        for d in range(4):
+        for d in (0, 2, 1, 3):
             nc.sync.dma_start(
                 w4_plane[:].bitcast(I32)[32 * d : 32 * d + 4, :], w4_dealt[:].bitcast(I32)[32 * d : 32 * (d + 1) : 4, :]
             )
         tab2 = load_words(tab2_words[0], "tab2")
         v2_rows = held([P, S], U8, "v2_rows")
         nc.vector.tensor_copy(v2_rows[:], tab2_rows[:].indirect(list2[:]))
-        for d in range(4):
-            nc.sync.dma_start(
-                v2_plane[:].bitcast(I32)[32 * d : 32 * d + 4, :], v2_rows[:].bitcast(I32)[32 * d : 32 * (d + 1) : 8, :]
-            )
+        for r in range(4):
+            nc.sync.dma_start(v2_plane[:].bitcast(I32)[r:P:32, :], v2_rows[:].bitcast(I32)[8 * r : P : 32, :])
         halves.append(load_w1_half(1))
         load_w4_words(1)
         tab = [load_words(tab_words[a], "tab%d" % a) for a in range(PASSES)]
@@ -161,7 +160,7 @@ def tile_list_tissue_share_scores_kernel(
             nc.vector.tensor_copy(v2[:, first : first + width], tab2[:].bitcast(U32).indirect(part))
             if first == QW:
                 deal_w4_words(1)
-        for d in range(4):
+        for d in (0, 2, 1, 3):
             row = 32 * d + PLANE_START
             nc.sync.dma_start(v_plane[:].bitcast(I32)[row : row + 4, :], v_rows[:].bitcast(I32)[32 * d : 32 * (d + 1) : 4, :])
         w1_raw[1, 1] = load_w1(1, 1)
@@ -344,11 +343,14 @@ def tile_list_tissue_share_scores_kernel(
             parts, cuts = factors
             result = reused([P, JW], F32, "result", tag)
             rows = dst.shape[1] // 2
-            for number, cols in enumerate(cuts[e]):
+            for cols in cuts[e]:
                 nc.vector.tensor_tensor(result[:, cols], pair[e][:, cols], parts[e][:, cols], ALU.mult)
-                count = rows // len(cuts[e])
-                row = rows * e + count * number
-                nc.sync.dma_start(dst[:, row : row + count, :], result[:, cols].rearrange("p (n c) -> p n c", n=count))
+                if len(cuts[e]) == 1:
+                    nc.sync.dma_start(dst[:, rows * e : rows * (e + 1), :], result[:].rearrange("p (n c) -> p n c", n=rows))
+                else:
+                    first = cols.start % QW
+                    row = dst[:, rows * e + cols.start // QW, :]
+                    nc.sync.dma_start(row[:, first : first + cols.stop - cols.start], result[:, cols])
 
         round_w1(0, 0, True)
         w1_bf[0, 1] = held([P, PACK * PASS], BF16, "w1_bf01")
@@ -437,7 +439,7 @@ def tile_list_tissue_share_scores_kernel(
         for q, tags in enumerate(((None, "w1_bf11"), (None, None))):
             pair = (third, fourth)[q]
             first = JW + quarter * q
-            factors = inverse(pair, tags, (whole, (whole, halved)[q]))
+            factors = inverse(pair, tags, ((whole, halved)[q], (whole, halved)[q]))
             pending.append((pair, factors, by_row[:, :, first : first + quarter]))
         for number, (pair, factors, dst) in enumerate(pending):
             for e in range(2):

@@ -321,7 +321,7 @@ def tile_list_tissue_share_scores_kernel(
                 stop=stop,
             )
 
-        def inverse(pair, tags, cuts):
+        def inverse(pair, tags, cuts, twice=False):
             size = ring.tile([P, 2, JW], F32, name="size")
             for e in range(2):
                 nc.scalar.activation(size[:, e, :], pair[e][:], ACT.Abs)
@@ -332,19 +332,24 @@ def tile_list_tissue_share_scores_kernel(
             for e in range(2):
                 if tags[e]:
                     parts.append(reused([P, JW], F32, "part", tags[e]))
-                    nc.gpsimd.tensor_tensor(parts[e][:], root[:, e, :], root[:, e, :], ALU.mult)
+                    for cols in cuts[e]:
+                        nc.gpsimd.tensor_tensor(parts[e][:, cols], root[:, e, cols], root[:, e, cols], ALU.mult)
                 else:
                     parts.append(ring.tile([P, JW], F32, name="part", bufs=5))
                     for cols in cuts[e]:
-                        nc.scalar.activation(parts[e][:, cols], root[:, e, cols], ACT.Square)
-            return parts, cuts
+                        if twice and e == 0 and cols.start == 0:
+                            nc.vector.tensor_tensor(parts[e][:, cols], pair[e][:, cols], root[:, e, cols], ALU.mult)
+                        else:
+                            nc.scalar.activation(parts[e][:, cols], root[:, e, cols], ACT.Square)
+            return parts, cuts, root if twice else None
 
         def score(pair, factors, dst, e, tag):
-            parts, cuts = factors
+            parts, cuts, root = factors
             result = reused([P, JW], F32, "result", tag)
             rows = dst.shape[1] // 2
             for cols in cuts[e]:
-                nc.vector.tensor_tensor(result[:, cols], pair[e][:, cols], parts[e][:, cols], ALU.mult)
+                left = root[:, e, :] if root and e == 0 and cols.start == 0 else pair[e]
+                nc.vector.tensor_tensor(result[:, cols], left[:, cols], parts[e][:, cols], ALU.mult)
                 if len(cuts[e]) == 1:
                     nc.sync.dma_start(dst[:, rows * e : rows * (e + 1), :], result[:].rearrange("p (n c) -> p n c", n=rows))
                 else:
@@ -436,11 +441,10 @@ def tile_list_tissue_share_scores_kernel(
         for u, tags in enumerate((("raw00", None), ("w1_bf00", "raw10"))):
             pair = first_half[2 * u : 2 * u + 2]
             pending.append((pair, inverse(pair, tags, (whole, whole)), by_row[:, 2 * u : 2 * u + 2, 0:JW]))
-        for q, tags in enumerate(((None, "w1_bf11"), (None, None))):
-            pair = (third, fourth)[q]
-            first = JW + quarter * q
-            factors = inverse(pair, tags, ((whole, halved)[q], (whole, halved)[q]))
-            pending.append((pair, factors, by_row[:, :, first : first + quarter]))
+        pending.append((third, inverse(third, (None, "w1_bf11"), (whole, halved)), by_row[:, :, JW : JW + quarter]))
         for number, (pair, factors, dst) in enumerate(pending):
             for e in range(2):
                 score(pair, factors, dst, e, homes[2 * number + e])
+        factors = inverse(fourth, (None, None), (halved, halved), True)
+        for e in range(2):
+            score(fourth, factors, by_row[:, :, JW + quarter : S], e, homes[6 + e])

from contextlib import ExitStack

import concourse.mybir as mybir
from concourse.masks import make_identity

K, K2, H, N, T, S = 1024, 512, 1024, 512, 2048, 1024
FLOPS = 2 * S * (K * H + K2 * H + H * N)

F32 = mybir.dt.float32
BF16 = mybir.dt.bfloat16
I32 = mybir.dt.int32
U32 = mybir.dt.uint32
U16 = mybir.dt.uint16
U8 = mybir.dt.uint8
FP8X4 = mybir.dt.float8_e4m3fn_x4
FP4X4 = mybir.dt.float4_e2m1fn_x4
ACT = mybir.ActivationFunctionType
ALU = mybir.AluOpType

P = 128
PACK = 4
PASS = P * PACK
JW = 512
QW = JW // 2
HALVES = S // JW
GROUPS = H // PASS
PASSES = K // PASS
PLANE_START = 4


def tile_list_tissue_share_scores_kernel(
    tc, tab_words, tab_scales, tab2_words, tab2_scales, offs, offs2, w1, w4_words, w4_scales, gain, w8_words, w8_scales, out
):
    nc = tc.nc
    with ExitStack() as ctx:
        keep = ctx.enter_context(tc.tile_pool(name="keep", bufs=1))
        ring = ctx.enter_context(tc.tile_pool(name="ring", bufs=2))
        laid = ctx.enter_context(tc.tile_pool(name="laid", bufs=1))
        psum = ctx.enter_context(tc.psum_pool(name="psum", bufs=1))

        def placed(shape, dtype, name, offset):
            return laid.tile(shape, dtype, name=name, align_bytes=64, offset=offset)

        def held(shape, dtype, name):
            return keep.tile(shape, dtype, name=name, align_bytes=64)

        def reused(shape, dtype, name, tag):
            return keep.tile(shape, dtype, name=name, tag=tag, align_bytes=64)

        lists = keep.tile([P, S // 16], U16, name="lists")
        list2 = keep.tile([P, S // 16], U16, name="list2")
        tab2_rows = held([P, T], U8, "tab2_rows")
        tab_rows = reused([P, T], U8, "tab_rows", "tab_rows")
        w4_rows = held([P, PASS], U8, "w4_rows")
        w4_plane = held([P, H], U8, "w4_plane")
        v2_plane = held([P, S], U8, "v2_plane")
        v_plane = held([P, PASSES * S], U8, "v_plane")
        w8_plane = held([P, N], U8, "w8_plane")
        warm = held([P, 2], F32, "warm")

        nc.gpsimd.memset(w4_rows[:].bitcast(I32), 0)
        nc.gpsimd.memset(tab2_rows[:].bitcast(I32), 0)
        nc.vector.memset(warm[:, 0:1], 0.0)
        nc.vector.memset(tab_rows[:].bitcast(I32), 0)
        nc.vector.memset(w4_plane[:].bitcast(I32), 0)
        nc.vector.memset(v2_plane[:].bitcast(I32), 0)
        nc.vector.memset(v_plane[:].bitcast(I32), 0)
        nc.vector.memset(w8_plane[:].bitcast(I32), 0)
        identity = held([P, P], F32, "identity")
        nc.vector.memset(identity[:], 0.0)
        make_identity(nc, identity[:], nomemset=True)
        nc.scalar.activation(warm[:, 1:2], warm[:, 0:1], ACT.Sigmoid)

        def load_w1(g, a):
            if (g, a) == (1, 1):
                raw = placed([P, PACK, PASS], F32, "raw11", 0)
            else:
                raw = reused([P, PACK, PASS], F32, "w1_raw", "raw%d%d" % (g, a))
            rows = w1[PASS * a : PASS * (a + 1), PASS * g : PASS * (g + 1)]
            by_row = rows.rearrange("(p j) c -> p j c", j=PACK)
            if (g, a) == (0, 0):
                return raw, by_row
            nc.sync.dma_start(raw[:], by_row)
            return raw

        def load_w1_half(u):
            raw = reused([P, PACK, QW], F32, "w1_half", "half%d" % u)
            rows = w1[PASS:K, QW * u : QW * (u + 1)]
            nc.sync.dma_start(raw[:], rows.rearrange("(p j) c -> p j c", j=PACK))
            return raw

        def load_words(words, tag):
            table = reused([P, T], I32, "table", tag)
            nc.sync.dma_start(table[:], words.rearrange("p t i -> p (t i)").bitcast(I32))
            return table

        w1_raw = {}
        w1_raw[0, 0], first_rows = load_w1(0, 0)
        nc.scalar.dma_start(w1_raw[0, 0][:, 0:2, :], first_rows[:, 0:2, :])
        nc.sync.dma_start(list2[:], offs2)
        nc.sync.dma_start(lists[:], offs)
        nc.sync.dma_start(
            w4_rows[:].bitcast(I32)[0:P:4, :], w4_scales.bitcast(I32)[0].rearrange("q (g c) -> (q g) c", g=GROUPS)
        )
        nc.sync.dma_start(tab2_rows[:].bitcast(I32)[0:P:8, :], tab2_scales.bitcast(I32)[0])
        nc.sync.dma_start(tab_rows[:].bitcast(I32)[0:P:4, :], tab_scales.bitcast(I32).rearrange("a q t -> q a t"))
        nc.sync.dma_start(w1_raw[0, 0][:, 2:4, :], first_rows[:, 2:4, :])
        w4_raw = {}

        def load_w4_words(g):
            w4_raw[g] = reused([P, 2 * PASS], U8, "w4_raw", "w4_raw%d" % g)
            nc.sync.dma_start(w4_raw[g][:].bitcast(I32), w4_words.bitcast(I32)[0, :, PASS // 2 * g : PASS // 2 * (g + 1)])

        load_w4_words(0)
        halves = [load_w1_half(0)]
        w4_dealt = held([P, PASS], U8, "w4_dealt")
        nc.vector.tensor_copy(
            w4_dealt[:].rearrange("p (t m) -> p t m", t=PACK), w4_rows[:].rearrange("p (m t) -> p t m", t=PACK)
        )
        for d in (0, 2, 1, 3):
            nc.sync.dma_start(
                w4_plane[:].bitcast(I32)[32 * d : 32 * d + 4, :], w4_dealt[:].bitcast(I32)[32 * d : 32 * (d + 1) : 4, :]
            )
        tab2 = load_words(tab2_words[0], "tab2")
        v2_rows = held([P, S], U8, "v2_rows")
        nc.vector.tensor_copy(v2_rows[:], tab2_rows[:].indirect(list2[:]))
        for r in range(4):
            nc.sync.dma_start(v2_plane[:].bitcast(I32)[r:P:32, :], v2_rows[:].bitcast(I32)[8 * r : P : 32, :])
        halves.append(load_w1_half(1))
        load_w4_words(1)
        tab = [load_words(tab_words[a], "tab%d" % a) for a in range(PASSES)]
        gains = {}

        def load_gains(g, first, count):
            part = held([P, count], F32, "gains%d%d" % (g, first))
            by_row = gain[PASS * g : PASS * (g + 1)].rearrange("(p t) -> p t", t=PACK)
            nc.sync.dma_start(part[:], by_row[:, first : first + count])
            for t in range(count):
                gains[g, first + t] = part[:, t : t + 1]

        load_gains(0, 0, 3)
        w1_raw[1, 0] = load_w1(1, 0)

        v_rows = held([P, S], U8, "v_rows")
        nc.vector.tensor_copy(v_rows[:], tab_rows[:].indirect(lists[:]))
        w4 = {}

        def deal_w4_words(g):
            w4[g] = held([P, 2 * PASS], U8, "w4_%d" % g)
            nc.scalar.copy(
                w4[g][:].bitcast(U16).rearrange("p (t m) -> p t m", t=PACK),
                w4_raw[g][:].bitcast(U16).rearrange("p (m t) -> p t m", t=PACK),
            )

        deal_w4_words(0)

        v2 = held([P, S], U32, "v2")
        for first, width in ((0, P), (P, P), (QW, QW), (JW, JW)):
            part = list2[:, first // 16 : (first + width) // 16]
            nc.vector.tensor_copy(v2[:, first : first + width], tab2[:].bitcast(U32).indirect(part))
            if first == QW:
                deal_w4_words(1)
        for d in (0, 2, 1, 3):
            row = 32 * d + PLANE_START
            nc.sync.dma_start(v_plane[:].bitcast(I32)[row : row + 4, :], v_rows[:].bitcast(I32)[32 * d : 32 * (d + 1) : 4, :])
        w1_raw[1, 1] = load_w1(1, 1)
        load_gains(0, 3, 1)
        load_gains(1, 0, PACK)
        w8 = held([P, GROUPS, N], I32, "w8")
        nc.sync.dma_start(w8[:], w8_words.rearrange("g p c i -> p g (c i)").bitcast(I32))
        for d in range(4):
            nc.sync.dma_start(
                w8_plane[:].bitcast(I32)[32 * d : 32 * d + 4 * GROUPS, :],
                w8_scales.bitcast(I32)[:, 4 * d : 4 * d + 4, :],
            )

        def bank(number):
            return psum.tile([P, JW], F32, name="bank", tag="bank%d" % number)

        w1_codes, w1_plane, w1_bf = {}, {}, {}

        def round_w1(g, a, on_scalar):
            grouped = reused([P, PACK * PASS], BF16, "grouped", "w1_bf%d%d" % (g, a))
            dst = grouped[:].rearrange("p (t m j) -> p m j t", t=PACK, j=PACK)
            src = w1_raw[g, a][:].rearrange("p j (m t) -> p m j t", t=PACK)
            if on_scalar:
                nc.scalar.copy(dst, src)
            else:
                nc.vector.tensor_copy(dst, src)
            w1_bf[g, a] = grouped

        def quantize_w1(g, a, tag):
            w1_codes[g, a] = reused([P, PASS], U32, "w1_codes", tag) if tag else placed([P, PASS], U32, "w1_codes10", 0)
            w1_plane[g, a] = held([P, PASS], U8, "w1_plane%d%d" % (g, a))
            nc.vector.quantize_mx(out=w1_codes[g, a][:].bitcast(FP8X4), scales=w1_plane[g, a][:], in_=w1_bf[g, a][:])

        pieces = [(g, half) for g in range(GROUPS) for half in range(HALVES)]
        unlike = {piece: reused([P, PACK, JW], F32, "unlike", "unlike%d%d" % piece) for piece in pieces[:3]}
        tissue = {piece: reused([P, PACK, JW], F32, "tissue", "tissue%d%d" % piece) for piece in pieces}
        across, turned = {}, {}

        def control_product_across(c):
            cols = slice(JW + P * c, JW + P * (c + 1))
            b = bank(c)
            nc.tensor.matmul_mx(
                out=b[:],
                lhsT=v2[:, cols].bitcast(FP8X4),
                lhsT_scale=v2_plane[:, cols],
                rhs=w4[1][:].bitcast(FP4X4),
                rhs_scale=w4_plane[:, PASS:H],
                start=True,
                stop=True,
            )
            across[c] = held([P, PACK, P], F32, "across%d" % c)
            nc.scalar.activation(across[c][:], b[:].rearrange("p (t m) -> p t m", t=PACK), ACT.Sigmoid, scale=-1.0)

        def turn(c):
            turned[c] = psum.tile([P, PACK, P], F32, name="turned", tag="bank%d" % (6 + c % 2))
            for t in range(PACK):
                nc.tensor.transpose(turned[c][:, t, :], across[c][:, t, :], identity[:])

        def control_product(g, half, t):
            cols = slice(JW * half, JW * (half + 1))
            col = PASS * g + P * t
            b = bank(t)
            nc.tensor.matmul_mx(
                out=b[:],
                lhsT=w4[g][:, 2 * P * t : 2 * P * (t + 1)].bitcast(FP4X4),
                lhsT_scale=w4_plane[:, col : col + P],
                rhs=v2[:, cols].bitcast(FP8X4),
                rhs_scale=v2_plane[:, cols],
                start=True,
                stop=True,
            )
            nc.scalar.activation(unlike[g, half][:, t, :], b[:], ACT.Sigmoid, scale=-1.0)

        def narrow_control_products(number, first, width, t0):
            b = bank(number)
            count = JW // width
            for e in range(count):
                t = t0 + e
                nc.tensor.matmul_mx(
                    out=b[:, width * e : width * (e + 1)],
                    lhsT=w4[0][:, 2 * P * t : 2 * P * (t + 1)].bitcast(FP4X4),
                    lhsT_scale=w4_plane[:, P * t : P * (t + 1)],
                    rhs=v2[:, first : first + width].bitcast(FP8X4),
                    rhs_scale=v2_plane[:, first : first + width],
                    start=True,
                    stop=True,
                )
            src = b[:].rearrange("p (e c) -> p e c", e=count)
            nc.scalar.activation(unlike[0, 0][:, t0 : t0 + count, first : first + width], src, ACT.Sigmoid, scale=-1.0)

        v = {}

        def gather_tissue_words(a):
            v[a] = held([P, S], U32, "v%d" % a)
            nc.vector.tensor_copy(v[a][:], tab[a][:].bitcast(U32).indirect(lists[:]))

        def tissue_product(g, half, t, number):
            cols = slice(JW * half, JW * (half + 1))
            rows = slice(P * t, P * (t + 1))
            acc = bank(number)
            for a in range(PASSES):
                nc.tensor.matmul_mx(
                    out=acc[:],
                    lhsT=w1_codes[g, a][:, rows].bitcast(FP8X4),
                    lhsT_scale=w1_plane[g, a][:, rows],
                    rhs=v[a][:, cols].bitcast(FP8X4),
                    rhs_scale=v_plane[PLANE_START:P, S * a + JW * half : S * a + JW * (half + 1)],
                    start=(a == 0),
                    stop=(a == PASSES - 1),
                )
            nc.scalar.activation(tissue[g, half][:, t, :], acc[:], ACT.Sigmoid)

        woven, h_codes, h_plane = {}, {}, {}

        def apply_gain(g, half, rows=range(PACK), dst=None):
            src = (tissue if (g, half) == (1, 1) else unlike)[g, half]
            for t in rows:
                nc.vector.tensor_scalar((dst or src)[:, t, :], src[:, t, :], gains[g, t], None, ALU.mult)

        def multiply(block, tag):
            g, first, width = block
            half, cols = first // JW, slice(first % JW, first % JW + width)
            woven[block] = reused([P, PACK * width], BF16, "woven", tag)
            nc.vector.tensor_tensor(
                woven[block][:].rearrange("p (c i t) -> p c t i", i=4, t=PACK),
                tissue[g, half][:, :, cols].rearrange("p t (c i) -> p c t i", i=4),
                unlike[g, half][:, :, cols].rearrange("p t (c i) -> p c t i", i=4),
                ALU.mult,
            )

        def multiply_turned(block, tag):
            g, first, width = block
            woven[block] = reused([P, PACK * width], BF16, "woven", tag)
            for e in range(2):
                c = (first - JW) // P + e
                nc.vector.tensor_tensor(
                    woven[block][:, PACK * P * e : PACK * P * (e + 1)].rearrange("p (c i t) -> p c t i", i=4, t=PACK),
                    turned[c][:].rearrange("p t (c i) -> p c t i", i=4),
                    tissue[1, 1][:, :, P * c : P * (c + 1)].rearrange("p t (c i) -> p c t i", i=4),
                    ALU.mult,
                )

        def quantize_h(block):
            h_codes[block] = held([P, block[2]], U32, "h_codes%d_%d" % block[:2])
            h_plane[block] = held([P, block[2]], U8, "h_plane%d_%d" % block[:2])
            nc.vector.quantize_mx(out=h_codes[block][:].bitcast(FP8X4), scales=h_plane[block][:], in_=woven[block][:])

        def last_pass(dst, n, block, first, width, start, stop):
            g = block[0]
            cols = slice(first - block[1], first - block[1] + width)
            nc.tensor.matmul_mx(
                out=dst,
                lhsT=w8[:, g, P * n : P * (n + 1)].bitcast(FP8X4),
                lhsT_scale=w8_plane[4 * g : P, P * n : P * (n + 1)],
                rhs=h_codes[block][:, cols].bitcast(FP8X4),
                rhs_scale=h_plane[block][:, cols],
                start=start,
                stop=stop,
            )

        def inverse(pair, tags, cuts, twice=False):
            size = ring.tile([P, 2, JW], F32, name="size")
            for e in range(2):
                nc.scalar.activation(size[:, e, :], pair[e][:], ACT.Abs)
            root = ring.tile([P, 2, JW], F32, name="root", bufs=3)
            for e in range(2):
                nc.scalar.activation(root[:, e, :], size[:, e, :], ACT.Abs_reciprocal_sqrt, bias=1.0)
            parts = []
            for e in range(2):
                if tags[e]:
                    parts.append(reused([P, JW], F32, "part", tags[e]))
                    for cols in cuts[e]:
                        nc.gpsimd.tensor_tensor(parts[e][:, cols], root[:, e, cols], root[:, e, cols], ALU.mult)
                else:
                    parts.append(ring.tile([P, JW], F32, name="part", bufs=5))
                    for cols in cuts[e]:
                        if twice and e == 0 and cols.start == 0:
                            nc.vector.tensor_tensor(parts[e][:, cols], pair[e][:, cols], root[:, e, cols], ALU.mult)
                        else:
                            nc.scalar.activation(parts[e][:, cols], root[:, e, cols], ACT.Square)
            return parts, cuts, root if twice else None

        def score(pair, factors, dst, e, tag):
            parts, cuts, root = factors
            result = reused([P, JW], F32, "result", tag)
            rows = dst.shape[1] // 2
            for cols in cuts[e]:
                left = root[:, e, :] if root and e == 0 and cols.start == 0 else pair[e]
                nc.vector.tensor_tensor(result[:, cols], left[:, cols], parts[e][:, cols], ALU.mult)
                if len(cuts[e]) == 1:
                    nc.sync.dma_start(dst[:, rows * e : rows * (e + 1), :], result[:].rearrange("p (n c) -> p n c", n=rows))
                else:
                    first = cols.start % QW
                    row = dst[:, rows * e + cols.start // QW, :]
                    nc.sync.dma_start(row[:, first : first + cols.stop - cols.start], result[:, cols])

        round_w1(0, 0, True)
        w1_bf[0, 1] = held([P, PACK * PASS], BF16, "w1_bf01")
        for u, copy in enumerate((nc.scalar.copy, nc.vector.tensor_copy)):
            dst = w1_bf[0, 1][:].rearrange("p (t m j) -> p m j t", t=PACK, j=PACK)[:, 64 * u : 64 * (u + 1)]
            copy(dst, halves[u][:].rearrange("p j (m t) -> p m j t", t=PACK))
        quantize_w1(0, 0, "w4_raw0")
        quantize_w1(0, 1, "tab2")
        for number, (first, width, t0) in enumerate(((0, P, 0), (P, P, 0), (QW, QW, 0), (QW, QW, 2))):
            narrow_control_products(number, first, width, t0)
        for g, half in ((1, 0), (0, 1)):
            for t in range(PACK):
                control_product(g, half, t)
        for c in range(4):
            control_product_across(c)
        nc.scalar.activation(unlike[0, 0][:, 2, :], unlike[0, 0][:, 2, :], ACT.Copy, scale=gains[0, 2])
        for a in range(PASSES):
            gather_tissue_words(a)
        round_w1(1, 0, False)
        apply_gain(0, 0, (0, 1))
        round_w1(1, 1, False)
        quantize_w1(1, 0, None)
        quantize_w1(1, 1, "w1_codes11")
        for t in range(PACK):
            tissue_product(0, 0, t, 4 + t)
        for t in range(2):
            tissue_product(0, 1, t, t)
        later = [(1, 0, t) for t in range(PACK)] + [(0, 1, 2), (0, 1, 3)] + [(1, 1, t) for t in range(PACK)]
        for number, (g, half, t) in enumerate(later):
            tissue_product(g, half, t, (2, 3, 6, 7)[number % 4])
        nc.scalar.activation(warm[:, 1:2], tissue[1, 1][:, PACK - 1, 0:1], ACT.Abs_reciprocal_sqrt, bias=1.0)

        quarter = JW // 2
        blocks = [(0, 0, JW), (1, 0, JW)] + [(g, JW + quarter * q, quarter) for q in range(2) for g in range(GROUPS)]
        woven_tags = ("w1_bf10", "w1_bf11")
        gained = placed([P, PACK, JW], F32, "gained01", 4 * PASS)
        apply_gain(0, 0, (3,))
        apply_gain(1, 0)
        multiply(blocks[0], woven_tags[0])
        apply_gain(0, 1, (0,), gained)
        quantize_h(blocks[0])
        apply_gain(0, 1, (1,), gained)
        multiply(blocks[1], woven_tags[1])
        apply_gain(0, 1, (2,), gained)
        quantize_h(blocks[1])
        apply_gain(0, 1, (3,), gained)
        unlike[0, 1] = gained

        by_row = out.rearrange("(n p) j -> p n j", p=P)
        whole, halved = (slice(0, JW),), (slice(0, QW), slice(QW, JW))
        pending = []
        first_half = [bank(n) for n in (0, 1, 4, 5)]
        for g in range(GROUPS):
            for n in range(N // P):
                last_pass(first_half[n][:], n, blocks[g], 0, JW, g == 0, g == 1)

        homes = ("tissue11", "tissue01", "unlike01", "tissue00", "tissue10", "unlike00", "unlike10", "tab0")

        def quarter_passes(pair, source, step):
            for n in range(N // P):
                dst = pair[n // 2][:, quarter * (n % 2) : quarter * (n % 2 + 1)]
                last_pass(dst, n, source, source[1], quarter, (step, n % 2) == (0, 0), (step, n % 2) == (1, 1))

        for c in range(2):
            turn(c)
        multiply(blocks[2], "raw00")
        apply_gain(1, 1)
        quantize_h(blocks[2])
        third = [bank(2), bank(3)]
        quarter_passes(third, blocks[2], 0)
        multiply_turned(blocks[3], "raw01")
        for c in range(2, 4):
            turn(c)
        quantize_h(blocks[3])
        quarter_passes(third, blocks[3], 1)
        multiply(blocks[4], "w1_bf00")
        quantize_h(blocks[4])
        multiply_turned(blocks[5], "raw10")
        fourth = [bank(6), bank(7)]
        quarter_passes(fourth, blocks[4], 0)
        quantize_h(blocks[5])
        quarter_passes(fourth, blocks[5], 1)
        for u, tags in enumerate((("raw00", None), ("w1_bf00", "raw10"))):
            pair = first_half[2 * u : 2 * u + 2]
            pending.append((pair, inverse(pair, tags, (whole, whole)), by_row[:, 2 * u : 2 * u + 2, 0:JW]))
        pending.append((third, inverse(third, (None, "w1_bf11"), (whole, halved)), by_row[:, :, JW : JW + quarter]))
        for number, (pair, factors, dst) in enumerate(pending):
            for e in range(2):
                score(pair, factors, dst, e, homes[2 * number + e])
        factors = inverse(fourth, (None, None), (halved, halved), True)
        for e in range(2):
            score(fourth, factors, by_row[:, :, JW + quarter : S], e, homes[6 + e])
